import numpy as np
import ml_dtypes


def mxq(x, axis, fmt="e4m3"):
    dtype, down = {"e4m3": (ml_dtypes.float8_e4m3fn, 7), "e5m2": (ml_dtypes.float8_e5m2, 14)}[fmt]
    v = np.moveaxis(np.asarray(x, np.float32).astype(ml_dtypes.bfloat16).astype(np.float64), axis, -1)
    blocks = v.reshape(v.shape[:-1] + (-1, 32))
    amax = np.abs(blocks).max(-1, keepdims=True)
    byte = np.maximum(np.where(amax > 0, np.frexp(amax)[1] - 1 + 127, 0) - down, 1)
    scale = np.exp2(byte - 127.0)
    codes = (blocks / scale).astype(np.float32).astype(dtype).astype(np.float64)
    return np.moveaxis((codes * scale).reshape(v.shape), -1, axis)


WIDE = False


def mx_kscale(k):
    if not WIDE:
        return np.ones(k)
    levels = np.array([10, -10, 5, -5, 0])
    if k % 512:
        return np.exp2(np.random.permutation(np.resize(levels, k // 32))).repeat(32)
    a = np.empty((k // 512, 16))
    for p in range(k // 512):
        a[p, :8] = np.random.permutation(np.resize(levels, 8))
        for g in range(8):
            far = levels[np.abs(levels - a[p, g]) >= 10]
            a[p, g + 8] = far[np.random.randint(len(far))]
    return np.exp2(a.ravel()).repeat(32)


def f64(x):
    return np.asarray(x).astype(np.float64)


def striped(idx):
    return np.tile(np.asarray(idx).reshape(-1, 16).T, (8, 1)).astype(np.uint16)


def unstriped(offs):
    return offs[:16].T.reshape(-1).astype(np.int64)


E2M1 = np.array([0.0, 0.5, 1.0, 1.5, 2.0, 3.0, 4.0, 6.0, -0.0, -0.5, -1.0, -1.5, -2.0, -3.0, -4.0, -6.0])


def pack_weight(w, fmt):
    k, n = w.shape
    w = f64(np.asarray(w, np.float32).astype(ml_dtypes.bfloat16)).reshape(k // 32, 32, n)
    amax = np.abs(w).max(1)
    if fmt == "e4m3":
        byte = np.frexp(amax)[1] - 1 + 127 - 7
    else:
        mant, ex = np.frexp(amax / 6.0)
        byte = np.where(mant > 0.5, ex, ex - 1) + 127
    byte = np.clip(np.where(amax > 0, byte, 1), 1, 254)
    scaled = (w * np.exp2(127.0 - byte)[:, None, :]).reshape(k, n).astype(np.float32)
    by_word = np.ascontiguousarray(scaled.reshape(k // 512, 128, 4, n).transpose(0, 1, 3, 2))
    if fmt == "e4m3":
        words = by_word.astype(ml_dtypes.float8_e4m3fn).view(np.uint8)
    else:
        c = by_word.astype(ml_dtypes.float4_e2m1fn).view(np.uint8) & 0xF
        words = (c[..., 0::2] | (c[..., 1::2] << 4)).reshape(k // 512, 128, 2 * n)
    return np.ascontiguousarray(words), np.ascontiguousarray(byte.astype(np.uint8).reshape(k // 512, 16, n))


def unpack_weight(words, scales, fmt):
    g, _, n = scales.shape
    words = np.ascontiguousarray(words).reshape(g, 128, n, -1)
    if fmt == "e4m3":
        vals = words.view(ml_dtypes.float8_e4m3fn).astype(np.float64)
    else:
        nib = np.empty((g, 128, n, 4), np.uint8)
        nib[..., 0::2] = words & 0xF
        nib[..., 1::2] = words >> 4
        vals = E2M1[nib]
    vals = vals * np.repeat(np.exp2(scales.astype(np.float64) - 127.0), 8, axis=1)[..., None]
    return vals.transpose(0, 1, 3, 2).reshape(g * 512, n)


B, N, T, D, NQ = 1, 512, 2048, 1024, 128
SEG = 32


def setup_inputs():
    n = np.random.standard_normal
    pages = np.random.permutation(T // 32)[:B * N // 32]
    idx = (pages[:, None] * 32 + np.arange(32)[None, :]).reshape(-1)
    pages2 = np.random.permutation(1024 // 32)[:B * N // 32]
    idx2 = (pages2[:, None] * 32 + np.arange(32)[None, :]).reshape(-1)
    s = mx_kscale(D)[:, None]
    kp = pack_weight(n((D, T)) / s, "e2m1")
    return {
        "uT": (n((B, D, NQ)) * s * (1.00 / np.sqrt(D))).astype(np.float32),
        "vT": (n((B, D, NQ)) * s * (1.00 / np.sqrt(D))).astype(np.float32),
        "k_words": np.ascontiguousarray(kp[0].reshape(1, 2, 128, T, 2).transpose(0, 2, 3, 1, 4)).reshape(1, 128, T, 4),
        "k_scales": kp[1],
        "cT": (n((D, 1024)) / s).astype(np.float32),
        "offs": striped(idx),
        "offs2": striped(idx2),
    }


def reference(uT, vT, k_words, k_scales, cT, offs, offs2):
    idx = unstriped(offs)
    idx2 = unstriped(offs2)
    pick = lambda x, which: x[:, which].reshape(x.shape[0], B, -1).transpose(1, 0, 2)
    k = unpack_weight(k_words.reshape(1, 128, T, 2, 2).transpose(0, 3, 1, 2, 4).reshape(2, 128, 2 * T), k_scales, "e2m1")
    kg = pick(k, idx)
    cg = mxq(pick(f64(cT), idx2), 1, "e4m3")
    uq = mxq(f64(uT), 1, "e4m3")
    vq = mxq(f64(vT), 1, "e4m3")
    a = (uq.transpose(0, 2, 1) @ kg) + (vq.transpose(0, 2, 1) @ cg)
    y = a.reshape(B, NQ, N // SEG, SEG).max(-1)
    return y

@@ -1,0 +1,149 @@
+from contextlib import ExitStack
+
+import concourse.mybir as mybir
+
+P = 128
+PACK = 4
+K_PASS = P * PACK
+D, T, C, NQ, SLOTS, SEG = 1024, 2048, 1024, 128, 512, 32
+PASSES = D // K_PASS
+BANK_N = 128
+BANKS = SLOTS // BANK_N
+RUN = 4
+
+FLOPS = 2 * 2 * D * NQ * SLOTS
+
+F32 = mybir.dt.float32
+BF16 = mybir.dt.bfloat16
+I32 = mybir.dt.int32
+U32 = mybir.dt.uint32
+U16 = mybir.dt.uint16
+U8 = mybir.dt.uint8
+FP8X4 = mybir.dt.float8_e4m3fn_x4
+FP4X4 = mybir.dt.float4_e2m1fn_x4
+
+
+def interleave(copy, grouped, planes):
+    copy(
+        out=grouped.rearrange("p (c i) t -> p c t i", i=RUN),
+        in_=planes.rearrange("p t (c i) -> p c t i", i=RUN),
+    )
+
+
+def tile_attend_txlseg_kernel(tc, uT, vT, k_words, k_scales, cT, offs, offs2, out):
+    nc = tc.nc
+    with ExitStack() as ctx:
+        sb = ctx.enter_context(tc.tile_pool(name="sb", bufs=1))
+        psum = ctx.enter_context(tc.psum_pool(name="psum", bufs=1))
+
+        key_list = sb.tile([P, SLOTS // 16], U16, name="key_list")
+        pos_list = sb.tile([P, SLOTS // 16], U16, name="pos_list")
+        ks_pool = sb.tile([P, PASSES, T // 4], I32, name="ks_pool", align_bytes=64)
+        kw_pool = sb.tile([P, T], I32, name="kw_pool", align_bytes=64)
+        nc.vector.memset(ks_pool[:], 0)
+
+        c_rows = cT.rearrange("(g p t) n -> g p t n", p=P, t=PACK)
+        loads = [(0, 0, 2), (0, 2, 2), (1, 0, 2), (1, 2, 1), (1, 3, 1)]
+        c_plane = {}
+        for g, t0, count in loads:
+            c_pool = sb.tile([P, count, C], F32, name=f"c_pool{g}{t0}", align_bytes=64)
+            nc.sync.dma_start(out=c_pool[:], in_=c_rows[g][:, t0 : t0 + count, :])
+            for t in range(count):
+                c_plane[g, t0 + t] = c_pool[:, t, :]
+            if (g, t0) == (0, 0):
+                nc.sync.dma_start(pos_list[:], offs2)
+            if (g, t0) == (0, 2):
+                nc.sync.dma_start(key_list[:], offs)
+        scale_rows = k_scales.rearrange("o (q r) t -> r q o t", r=4)
+        for r in range(4):
+            nc.gpsimd.dma_start(out=ks_pool[r:P:32, :, :], in_=scale_rows[r].bitcast(I32))
+        nc.sync.dma_start(out=kw_pool[:], in_=k_words[0].rearrange("p t b -> p (t b)").bitcast(I32))
+        q_raw = []
+        for name, queries in (("v", vT), ("u", uT)):
+            rows = queries[0].rearrange("(g p t) q -> g p t q", p=P, t=PACK)
+            for g in range(PASSES):
+                raw = sb.tile([P, PACK, NQ], F32, name=f"{name}_raw{g}", align_bytes=64)
+                nc.sync.dma_start(out=raw[:], in_=rows[g])
+                q_raw.append(raw)
+
+        def quantize(name, grouped, width):
+            codes = sb.tile([P, width], U32, name=f"{name}_codes", align_bytes=64)
+            scales = sb.tile([P, width], U8, name=f"{name}_scales", align_bytes=64)
+            nc.vector.quantize_mx(out=codes[:].bitcast(FP8X4), scales=scales[:], in_=grouped)
+            return codes, scales
+
+        def gather_plane(picked, g, t, s0, s1):
+            nc.vector.tensor_copy(
+                out=picked[:, t, s0:s1], in_=c_plane[g, t].indirect(pos_list[:, s0 // 16 : s1 // 16])
+            )
+
+        picked0 = sb.tile([P, PACK, SLOTS], F32, name="picked0", align_bytes=64)
+        picked1 = sb.tile([P, PACK, SLOTS], F32, name="picked1", tag="picked1", align_bytes=64)
+        grouped0 = sb.tile([P, SLOTS, PACK], BF16, name="grouped0", align_bytes=64)
+        grouped1 = sb.tile([P, SLOTS, PACK], BF16, name="grouped1", tag="grouped1", align_bytes=64)
+        ks = sb.tile([P, PASSES, SLOTS], U8, name="ks", align_bytes=64)
+        ks_bytes = ks_pool[:].bitcast(U8)
+        half = SLOTS // 2
+        for t in range(PACK):
+            gather_plane(picked0, 0, t, 0, SLOTS)
+        interleave(nc.scalar.copy, grouped0[:], picked0[:])
+        for g in range(PASSES):
+            nc.vector.tensor_copy(out=ks[:, g, :], in_=ks_bytes[:, g, :].indirect(key_list[:]))
+        gather_plane(picked1, 1, 0, 0, SLOTS)
+        gather_plane(picked1, 1, 1, 0, SLOTS)
+        gather_plane(picked1, 1, 2, 0, SLOTS)
+        c_mx = [quantize("c0", grouped0[:].rearrange("p n t -> p (n t)"), SLOTS)]
+        gather_plane(picked1, 1, 3, 0, half)
+        gather_plane(picked1, 1, 3, half, SLOTS)
+        interleave(nc.scalar.copy, grouped1[:, :half, :], picked1[:, :, :half])
+        interleave(nc.vector.tensor_copy, grouped1[:, half:, :], picked1[:, :, half:])
+        c_mx.append(quantize("c1", grouped1[:].rearrange("p n t -> p (n t)"), SLOTS))
+
+        kw_pairs = sb.tile([P, SLOTS], U32, name="kw_pairs", tag="grouped1", align_bytes=64)
+        nc.vector.tensor_copy(out=kw_pairs[:], in_=kw_pool[:].bitcast(U32).indirect(key_list[:]))
+        kw = sb.tile([P, PASSES, 2 * SLOTS], U8, name="kw", align_bytes=64)
+        nc.vector.tensor_copy(
+            out=kw[:].bitcast(U16),
+            in_=kw_pairs[:].bitcast(U16).rearrange("p (n o) -> p o n", o=PASSES),
+        )
+
+        q_grouped = sb.tile([P, 2 * PASSES, NQ, PACK], BF16, name="q_grouped", tag="picked1", align_bytes=64)
+        q_mx = []
+        for j, raw in enumerate(q_raw):
+            interleave(nc.scalar.copy, q_grouped[:, j, :, :], raw[:])
+            q_mx.append(quantize(f"q{j}", q_grouped[:, j, :, :].rearrange("p q t -> p (q t)"), NQ))
+
+        acc = [psum.tile([P, BANK_N], F32, name=f"acc{b}") for b in range(BANKS)]
+        for g in range(PASSES):
+            for b in range(BANKS):
+                cols = slice(b * BANK_N, (b + 1) * BANK_N)
+                nc.tensor.matmul_mx(
+                    out=acc[b][:],
+                    lhsT=q_mx[g][0][:].bitcast(FP8X4),
+                    lhsT_scale=q_mx[g][1][:],
+                    rhs=c_mx[g][0][:, cols].bitcast(FP8X4),
+                    rhs_scale=c_mx[g][1][:, cols],
+                    start=(g == 0),
+                    stop=False,
+                )
+        best = sb.tile([P, SLOTS // SEG], F32, name="best")
+        pages = BANK_N // SEG
+        for g in range(PASSES):
+            for b in range(BANKS):
+                nc.tensor.matmul_mx(
+                    out=acc[b][:],
+                    lhsT=q_mx[PASSES + g][0][:].bitcast(FP8X4),
+                    lhsT_scale=q_mx[PASSES + g][1][:],
+                    rhs=kw[:, g, 2 * b * BANK_N : 2 * (b + 1) * BANK_N].bitcast(FP4X4),
+                    rhs_scale=ks[:, g, b * BANK_N : (b + 1) * BANK_N],
+                    start=False,
+                    stop=(g == PASSES - 1),
+                )
+        for b in range(BANKS):
+            nc.vector.tensor_reduce(
+                out=best[:, b * pages : (b + 1) * pages],
+                in_=acc[b][:].rearrange("p (j s) -> p j s", s=SEG),
+                axis=mybir.AxisListType.X,
+                op=mybir.AluOpType.max,
+            )
+        nc.sync.dma_start(out=out[0], in_=best[:])

@@ -39,32 +39,23 @@ def tile_attend_txlseg_kernel(tc, uT, vT, k_words, k_scales, cT, offs, offs2, ou
         key_list = sb.tile([P, SLOTS // 16], U16, name="key_list")
         pos_list = sb.tile([P, SLOTS // 16], U16, name="pos_list")
         ks_pool = sb.tile([P, PASSES, T // 4], I32, name="ks_pool", align_bytes=64)
-        kw_pool = sb.tile([P, T], I32, name="kw_pool", align_bytes=64)
         nc.vector.memset(ks_pool[:], 0)
 
         c_rows = cT.rearrange("(g p t) n -> g p t n", p=P, t=PACK)
-        loads = [(0, 0, 2), (0, 2, 2), (1, 0, 2), (1, 2, 1), (1, 3, 1)]
+        loads = [(0, 0, 1), (0, 1, 1), (0, 2, 2), (1, 0, 2), (1, 2, 1), (1, 3, 1)]
         c_plane = {}
         for g, t0, count in loads:
-            c_pool = sb.tile([P, count, C], F32, name=f"c_pool{g}{t0}", align_bytes=64)
+            c_pool = sb.tile([P, count, C], F32, name=f"c_pool{g}{t0}", tag=f"c_pool{g}{t0}", align_bytes=64)
             nc.sync.dma_start(out=c_pool[:], in_=c_rows[g][:, t0 : t0 + count, :])
             for t in range(count):
                 c_plane[g, t0 + t] = c_pool[:, t, :]
             if (g, t0) == (0, 0):
                 nc.sync.dma_start(pos_list[:], offs2)
-            if (g, t0) == (0, 2):
+            if (g, t0) == (0, 1):
                 nc.sync.dma_start(key_list[:], offs)
         scale_rows = k_scales.rearrange("o (q r) t -> r q o t", r=4)
         for r in range(4):
-            nc.gpsimd.dma_start(out=ks_pool[r:P:32, :, :], in_=scale_rows[r].bitcast(I32))
-        nc.sync.dma_start(out=kw_pool[:], in_=k_words[0].rearrange("p t b -> p (t b)").bitcast(I32))
-        q_raw = []
-        for name, queries in (("v", vT), ("u", uT)):
-            rows = queries[0].rearrange("(g p t) q -> g p t q", p=P, t=PACK)
-            for g in range(PASSES):
-                raw = sb.tile([P, PACK, NQ], F32, name=f"{name}_raw{g}", align_bytes=64)
-                nc.sync.dma_start(out=raw[:], in_=rows[g])
-                q_raw.append(raw)
+            nc.scalar.dma_start(out=ks_pool[r:P:32, :, :], in_=scale_rows[r].bitcast(I32))
 
         def quantize(name, grouped, width):
             codes = sb.tile([P, width], U32, name=f"{name}_codes", align_bytes=64)
@@ -86,6 +77,13 @@ def tile_attend_txlseg_kernel(tc, uT, vT, k_words, k_scales, cT, offs, offs2, ou
         half = SLOTS // 2
         for t in range(PACK):
             gather_plane(picked0, 0, t, 0, SLOTS)
+        kw_pool = sb.tile([P, T], I32, name="kw_pool", tag="c_pool00", align_bytes=64)
+        nc.sync.dma_start(out=kw_pool[:], in_=k_words[0].rearrange("p t b -> p (t b)").bitcast(I32))
+        q_raw = sb.tile([P, 2 * PASSES, PACK, NQ], F32, name="q_raw", tag="c_pool02", align_bytes=64)
+        for j, queries in enumerate((vT, uT)):
+            rows = queries[0].rearrange("(g p t) q -> g p t q", p=P, t=PACK)
+            for g in range(PASSES):
+                nc.sync.dma_start(out=q_raw[:, j * PASSES + g, :, :], in_=rows[g])
         interleave(nc.scalar.copy, grouped0[:], picked0[:])
         for g in range(PASSES):
             nc.vector.tensor_copy(out=ks[:, g, :], in_=ks_bytes[:, g, :].indirect(key_list[:]))
@@ -109,8 +107,8 @@ def tile_attend_txlseg_kernel(tc, uT, vT, k_words, k_scales, cT, offs, offs2, ou
 
         q_grouped = sb.tile([P, 2 * PASSES, NQ, PACK], BF16, name="q_grouped", tag="picked1", align_bytes=64)
         q_mx = []
-        for j, raw in enumerate(q_raw):
-            interleave(nc.scalar.copy, q_grouped[:, j, :, :], raw[:])
+        for j in range(2 * PASSES):
+            interleave(nc.scalar.copy, q_grouped[:, j, :, :], q_raw[:, j, :, :])
             q_mx.append(quantize(f"q{j}", q_grouped[:, j, :, :].rearrange("p q t -> p (q t)"), NQ))
 
         acc = [psum.tile([P, BANK_N], F32, name=f"acc{b}") for b in range(BANKS)]

@@ -10,6 +10,7 @@ PASSES = D // K_PASS
 BANK_N = 128
 BANKS = SLOTS // BANK_N
 RUN = 4
+PLANE_BYTES = 4 * C
 
 FLOPS = 2 * 2 * D * NQ * SLOTS
 
@@ -34,33 +35,39 @@ def tile_attend_txlseg_kernel(tc, uT, vT, k_words, k_scales, cT, offs, offs2, ou
     nc = tc.nc
     with ExitStack() as ctx:
         sb = ctx.enter_context(tc.tile_pool(name="sb", bufs=1))
+        stage = ctx.enter_context(tc.tile_pool(name="stage", bufs=1))
         psum = ctx.enter_context(tc.psum_pool(name="psum", bufs=1))
 
         key_list = sb.tile([P, SLOTS // 16], U16, name="key_list")
         pos_list = sb.tile([P, SLOTS // 16], U16, name="pos_list")
         ks_pool = sb.tile([P, PASSES, T // 4], I32, name="ks_pool", align_bytes=64)
         nc.vector.memset(ks_pool[:], 0)
-
-        c_rows = cT.rearrange("(g p t) n -> g p t n", p=P, t=PACK)
-        loads = [(0, 0, 1), (0, 1, 1), (0, 2, 2), (1, 0, 2), (1, 2, 1), (1, 3, 1)]
-        c_plane = {}
-        for g, t0, count in loads:
-            c_pool = sb.tile([P, count, C], F32, name=f"c_pool{g}{t0}", tag=f"c_pool{g}{t0}", align_bytes=64)
-            nc.sync.dma_start(out=c_pool[:], in_=c_rows[g][:, t0 : t0 + count, :])
-            for t in range(count):
-                c_plane[g, t0 + t] = c_pool[:, t, :]
-            if (g, t0) == (0, 0):
-                nc.sync.dma_start(pos_list[:], offs2)
-            if (g, t0) == (0, 1):
-                nc.sync.dma_start(key_list[:], offs)
+        nc.sync.dma_start(pos_list[:], offs2)
+        nc.sync.dma_start(key_list[:], offs)
         scale_rows = k_scales.rearrange("o (q r) t -> r q o t", r=4)
         for r in range(4):
             nc.scalar.dma_start(out=ks_pool[r:P:32, :, :], in_=scale_rows[r].bitcast(I32))
 
+        c_rows = cT.rearrange("(g p t) n -> g p t n", p=P, t=PACK)
+        c_plane = {}
+
+        def load_planes(g, t0, count, at):
+            c_pool = stage.tile([P, count, C], F32, name=f"c_pool{g}{t0}", offset=at * PLANE_BYTES, align_bytes=64)
+            nc.sync.dma_start(out=c_pool[:], in_=c_rows[g][:, t0 : t0 + count, :])
+            for t in range(count):
+                c_plane[g, t0 + t] = c_pool[:, t, :]
+
+        def load_queries(name, queries, at, step):
+            raw = stage.tile([P, PASSES, PACK, NQ], F32, name=name, offset=at * PLANE_BYTES, align_bytes=64)
+            rows = queries[0].rearrange("(g p t) q -> p g t q", p=P, t=PACK)
+            for g in range(0, PASSES, step):
+                nc.sync.dma_start(out=raw[:, g : g + step, :, :], in_=rows[:, g : g + step, :, :])
+            return raw
+
         def quantize(name, grouped, width):
             codes = sb.tile([P, width], U32, name=f"{name}_codes", align_bytes=64)
             scales = sb.tile([P, width], U8, name=f"{name}_scales", align_bytes=64)
-            nc.vector.quantize_mx(out=codes[:].bitcast(FP8X4), scales=scales[:], in_=grouped)
+            nc.vector.quantize_mx(out=codes[:].bitcast(FP8X4), scales=scales[:], in_=grouped.rearrange("p n t -> p (n t)"))
             return codes, scales
 
         def gather_plane(picked, g, t, s0, s1):
@@ -68,48 +75,55 @@ def tile_attend_txlseg_kernel(tc, uT, vT, k_words, k_scales, cT, offs, offs2, ou
                 out=picked[:, t, s0:s1], in_=c_plane[g, t].indirect(pos_list[:, s0 // 16 : s1 // 16])
             )
 
+        load_planes(0, 0, 2, 0)
+        load_planes(0, 2, 2, 2)
+        load_planes(1, 0, 2, 4)
+        load_planes(1, 2, 1, 6)
+
         picked0 = sb.tile([P, PACK, SLOTS], F32, name="picked0", align_bytes=64)
-        picked1 = sb.tile([P, PACK, SLOTS], F32, name="picked1", tag="picked1", align_bytes=64)
+        picked1 = sb.tile([P, PACK, SLOTS], F32, name="picked1", tag="late0", align_bytes=64)
         grouped0 = sb.tile([P, SLOTS, PACK], BF16, name="grouped0", align_bytes=64)
-        grouped1 = sb.tile([P, SLOTS, PACK], BF16, name="grouped1", tag="grouped1", align_bytes=64)
+        grouped1 = sb.tile([P, SLOTS, PACK], BF16, name="grouped1", tag="late1", align_bytes=64)
         ks = sb.tile([P, PASSES, SLOTS], U8, name="ks", align_bytes=64)
         ks_bytes = ks_pool[:].bitcast(U8)
         half = SLOTS // 2
-        for t in range(PACK):
-            gather_plane(picked0, 0, t, 0, SLOTS)
-        kw_pool = sb.tile([P, T], I32, name="kw_pool", tag="c_pool00", align_bytes=64)
-        nc.sync.dma_start(out=kw_pool[:], in_=k_words[0].rearrange("p t b -> p (t b)").bitcast(I32))
-        q_raw = sb.tile([P, 2 * PASSES, PACK, NQ], F32, name="q_raw", tag="c_pool02", align_bytes=64)
-        for j, queries in enumerate((vT, uT)):
-            rows = queries[0].rearrange("(g p t) q -> g p t q", p=P, t=PACK)
-            for g in range(PASSES):
-                nc.sync.dma_start(out=q_raw[:, j * PASSES + g, :, :], in_=rows[g])
-        interleave(nc.scalar.copy, grouped0[:], picked0[:])
+        gather_plane(picked0, 0, 0, 0, SLOTS)
+        gather_plane(picked0, 0, 1, 0, SLOTS)
+        load_planes(1, 3, 1, 0)
+        v_raw = load_queries("v_raw", vT, 1, PASSES)
         for g in range(PASSES):
             nc.vector.tensor_copy(out=ks[:, g, :], in_=ks_bytes[:, g, :].indirect(key_list[:]))
+        gather_plane(picked0, 0, 2, 0, SLOTS)
+        gather_plane(picked0, 0, 3, 0, SLOTS)
+        kw_pool = stage.tile([P, T], I32, name="kw_pool", offset=2 * PLANE_BYTES, align_bytes=64)
+        nc.sync.dma_start(out=kw_pool[:], in_=k_words[0].rearrange("p t b -> p (t b)").bitcast(I32))
+        interleave(nc.scalar.copy, grouped0[:], picked0[:])
         gather_plane(picked1, 1, 0, 0, SLOTS)
         gather_plane(picked1, 1, 1, 0, SLOTS)
+        u_raw = load_queries("u_raw", uT, 4, 1)
         gather_plane(picked1, 1, 2, 0, SLOTS)
-        c_mx = [quantize("c0", grouped0[:].rearrange("p n t -> p (n t)"), SLOTS)]
+        c_mx = [quantize("c0", grouped0[:], SLOTS)]
         gather_plane(picked1, 1, 3, 0, half)
         gather_plane(picked1, 1, 3, half, SLOTS)
         interleave(nc.scalar.copy, grouped1[:, :half, :], picked1[:, :, :half])
         interleave(nc.vector.tensor_copy, grouped1[:, half:, :], picked1[:, :, half:])
-        c_mx.append(quantize("c1", grouped1[:].rearrange("p n t -> p (n t)"), SLOTS))
+        c_mx.append(quantize("c1", grouped1[:], SLOTS))
 
-        kw_pairs = sb.tile([P, SLOTS], U32, name="kw_pairs", tag="grouped1", align_bytes=64)
+        v_grouped = sb.tile([P, PASSES, NQ, PACK], BF16, name="v_grouped", tag="late0", align_bytes=64)
+        q_mx = []
+        for g in range(PASSES):
+            interleave(nc.scalar.copy, v_grouped[:, g, :, :], v_raw[:, g, :, :])
+            q_mx.append(quantize(f"v{g}", v_grouped[:, g, :, :], NQ))
+
+        kw_pairs = sb.tile([P, SLOTS], U32, name="kw_pairs", tag="late0", align_bytes=64)
         nc.vector.tensor_copy(out=kw_pairs[:], in_=kw_pool[:].bitcast(U32).indirect(key_list[:]))
         kw = sb.tile([P, PASSES, 2 * SLOTS], U8, name="kw", align_bytes=64)
-        nc.vector.tensor_copy(
-            out=kw[:].bitcast(U16),
-            in_=kw_pairs[:].bitcast(U16).rearrange("p (n o) -> p o n", o=PASSES),
-        )
-
-        q_grouped = sb.tile([P, 2 * PASSES, NQ, PACK], BF16, name="q_grouped", tag="picked1", align_bytes=64)
-        q_mx = []
-        for j in range(2 * PASSES):
-            interleave(nc.scalar.copy, q_grouped[:, j, :, :], q_raw[:, j, :, :])
-            q_mx.append(quantize(f"q{j}", q_grouped[:, j, :, :].rearrange("p q t -> p (q t)"), NQ))
+        u_grouped = sb.tile([P, PASSES, NQ, PACK], BF16, name="u_grouped", tag="late1", align_bytes=64)
+        halves = kw_pairs[:].bitcast(U16).rearrange("p (n o) -> p o n", o=PASSES)
+        for g in range(PASSES):
+            nc.vector.tensor_copy(out=kw[:, g, :].bitcast(U16), in_=halves[:, g, :])
+            interleave(nc.scalar.copy, u_grouped[:, g, :, :], u_raw[:, g, :, :])
+            q_mx.append(quantize(f"u{g}", u_grouped[:, g, :, :], NQ))
 
         acc = [psum.tile([P, BANK_N], F32, name=f"acc{b}") for b in range(BANKS)]
         for g in range(PASSES):

@@ -10,7 +10,13 @@ PASSES = D // K_PASS
 BANK_N = 128
 BANKS = SLOTS // BANK_N
 RUN = 4
-PLANE_BYTES = 4 * C
+STAGE_AT = {
+    "c4": 0, "c0": 4, "c5": 8,
+    "c6": 16, "c1": 21, "ks_both": 24, "c7": 25,
+    "v0": 33, "c2": 35, "kw_pool": 37,
+    "v1": 53, "c3": 55, "u0": 57, "u1": 61,
+    "grouped1": 66, "kw": 72, "picked1": 74, "v1_grouped": 74, "u_grouped": 78,
+}
 
 FLOPS = 2 * 2 * D * NQ * SLOTS
 
@@ -38,30 +44,19 @@ def tile_attend_txlseg_kernel(tc, uT, vT, k_words, k_scales, cT, offs, offs2, ou
         stage = ctx.enter_context(tc.tile_pool(name="stage", bufs=1))
         psum = ctx.enter_context(tc.psum_pool(name="psum", bufs=1))
 
-        key_list = sb.tile([P, SLOTS // 16], U16, name="key_list")
-        pos_list = sb.tile([P, SLOTS // 16], U16, name="pos_list")
-        ks_pool = sb.tile([P, PASSES, T // 4], I32, name="ks_pool", align_bytes=64)
-        nc.vector.memset(ks_pool[:], 0)
-        nc.sync.dma_start(pos_list[:], offs2)
-        nc.sync.dma_start(key_list[:], offs)
-        scale_rows = k_scales.rearrange("o (q r) t -> r q o t", r=4)
-        for r in range(4):
-            nc.scalar.dma_start(out=ks_pool[r:P:32, :, :], in_=scale_rows[r].bitcast(I32))
+        def staged(name, shape, dtype):
+            return stage.tile(shape, dtype, name=name, offset=STAGE_AT[name] * 512, align_bytes=64)
 
-        c_rows = cT.rearrange("(g p t) n -> g p t n", p=P, t=PACK)
-        c_plane = {}
+        c_rows = cT.rearrange("(g p t) n -> g t p n", p=P, t=PACK)
+        c_pool = {}
 
-        def load_planes(g, t0, count, at):
-            c_pool = stage.tile([P, count, C], F32, name=f"c_pool{g}{t0}", offset=at * PLANE_BYTES, align_bytes=64)
-            nc.sync.dma_start(out=c_pool[:], in_=c_rows[g][:, t0 : t0 + count, :])
-            for t in range(count):
-                c_plane[g, t0 + t] = c_pool[:, t, :]
+        def load_plane(j):
+            c_pool[j] = staged(f"c{j}", [P, C], F32)
+            nc.sync.dma_start(out=c_pool[j][:], in_=c_rows[j // PACK, j % PACK])
 
-        def load_queries(name, queries, at, step):
-            raw = stage.tile([P, PASSES, PACK, NQ], F32, name=name, offset=at * PLANE_BYTES, align_bytes=64)
-            rows = queries[0].rearrange("(g p t) q -> p g t q", p=P, t=PACK)
-            for g in range(0, PASSES, step):
-                nc.sync.dma_start(out=raw[:, g : g + step, :, :], in_=rows[:, g : g + step, :, :])
+        def load_queries(name, queries, g):
+            raw = staged(f"{name}{g}", [P, PACK, NQ], F32)
+            nc.sync.dma_start(out=raw[:], in_=queries[0].rearrange("(g p t) q -> g p t q", p=P, t=PACK)[g])
             return raw
 
         def quantize(name, grouped, width):
@@ -70,59 +65,72 @@ def tile_attend_txlseg_kernel(tc, uT, vT, k_words, k_scales, cT, offs, offs2, ou
             nc.vector.quantize_mx(out=codes[:].bitcast(FP8X4), scales=scales[:], in_=grouped.rearrange("p n t -> p (n t)"))
             return codes, scales
 
-        def gather_plane(picked, g, t, s0, s1):
+        def gather_plane(picked, j, s0, s1):
             nc.vector.tensor_copy(
-                out=picked[:, t, s0:s1], in_=c_plane[g, t].indirect(pos_list[:, s0 // 16 : s1 // 16])
+                out=picked[:, j % PACK, s0:s1], in_=c_pool[j][:].indirect(pos_list[:, s0 // 16 : s1 // 16])
             )
 
-        load_planes(0, 0, 2, 0)
-        load_planes(0, 2, 2, 2)
-        load_planes(1, 0, 2, 4)
-        load_planes(1, 2, 1, 6)
+        key_list = sb.tile([P, SLOTS // 16], U16, name="key_list")
+        pos_list = sb.tile([P, SLOTS // 16], U16, name="pos_list")
+        ks_pool = sb.tile([P, T // 4], I32, name="ks_pool", align_bytes=64)
+        ks_second = sb.tile([P, SLOTS // 4], I32, name="ks_second", align_bytes=64)
+        nc.vector.memset(ks_pool[:], 0)
+        nc.vector.memset(ks_second[:], 0)
+        load_plane(0)
+        nc.sync.dma_start(pos_list[:], offs2)
+        load_plane(1)
+        scale_rows = k_scales.rearrange("o (q r) t -> r q o t", r=4)
+        for r in range(4):
+            nc.sync.dma_start(out=ks_pool[r:P:16, :], in_=scale_rows[r].bitcast(I32))
+        load_plane(2)
+        nc.sync.dma_start(key_list[:], offs)
+        load_plane(3)
 
-        picked0 = sb.tile([P, PACK, SLOTS], F32, name="picked0", align_bytes=64)
-        picked1 = sb.tile([P, PACK, SLOTS], F32, name="picked1", tag="late0", align_bytes=64)
+        picked0 = sb.tile([P, PACK, SLOTS], F32, name="picked0", tag="picked0", align_bytes=64)
+        picked1 = staged("picked1", [P, PACK, SLOTS], F32)
         grouped0 = sb.tile([P, SLOTS, PACK], BF16, name="grouped0", align_bytes=64)
-        grouped1 = sb.tile([P, SLOTS, PACK], BF16, name="grouped1", tag="late1", align_bytes=64)
-        ks = sb.tile([P, PASSES, SLOTS], U8, name="ks", align_bytes=64)
-        ks_bytes = ks_pool[:].bitcast(U8)
+        grouped1 = staged("grouped1", [P, SLOTS, PACK], BF16)
         half = SLOTS // 2
-        gather_plane(picked0, 0, 0, 0, SLOTS)
-        gather_plane(picked0, 0, 1, 0, SLOTS)
-        load_planes(1, 3, 1, 0)
-        v_raw = load_queries("v_raw", vT, 1, PASSES)
-        for g in range(PASSES):
-            nc.vector.tensor_copy(out=ks[:, g, :], in_=ks_bytes[:, g, :].indirect(key_list[:]))
-        gather_plane(picked0, 0, 2, 0, SLOTS)
-        gather_plane(picked0, 0, 3, 0, SLOTS)
-        kw_pool = stage.tile([P, T], I32, name="kw_pool", offset=2 * PLANE_BYTES, align_bytes=64)
+        gather_plane(picked0, 0, 0, SLOTS)
+        load_plane(4)
+        load_plane(5)
+        gather_plane(picked0, 1, 0, SLOTS)
+        load_plane(6)
+        load_plane(7)
+        ks_both = staged("ks_both", [P, SLOTS], U8)
+        nc.vector.tensor_copy(out=ks_both[:], in_=ks_pool[:].bitcast(U8).indirect(key_list[:]))
+        nc.sync.dma_start(out=ks_second[0 : P - 16, :], in_=ks_both[16:P, :].bitcast(I32))
+        ks = [ks_both[:], ks_second[:].bitcast(U8)]
+        gather_plane(picked0, 2, 0, SLOTS)
+        v0_raw = load_queries("v", vT, 0)
+        kw_pool = staged("kw_pool", [P, T], I32)
         nc.sync.dma_start(out=kw_pool[:], in_=k_words[0].rearrange("p t b -> p (t b)").bitcast(I32))
+        gather_plane(picked0, 3, 0, SLOTS)
+        late_raw = [load_queries("v", vT, 1), load_queries("u", uT, 0), load_queries("u", uT, 1)]
         interleave(nc.scalar.copy, grouped0[:], picked0[:])
-        gather_plane(picked1, 1, 0, 0, SLOTS)
-        gather_plane(picked1, 1, 1, 0, SLOTS)
-        u_raw = load_queries("u_raw", uT, 4, 1)
-        gather_plane(picked1, 1, 2, 0, SLOTS)
+        for j in (4, 5, 6):
+            gather_plane(picked1, j, 0, SLOTS)
         c_mx = [quantize("c0", grouped0[:], SLOTS)]
-        gather_plane(picked1, 1, 3, 0, half)
-        gather_plane(picked1, 1, 3, half, SLOTS)
+        v0_grouped = sb.tile([P, NQ, PACK], BF16, name="v0_grouped", tag="picked0", align_bytes=64)
+        interleave(nc.scalar.copy, v0_grouped[:], v0_raw[:])
+        gather_plane(picked1, 7, 0, half)
         interleave(nc.scalar.copy, grouped1[:, :half, :], picked1[:, :, :half])
+        gather_plane(picked1, 7, half, SLOTS)
+        q_mx = [quantize("v0", v0_grouped[:], NQ)]
         interleave(nc.vector.tensor_copy, grouped1[:, half:, :], picked1[:, :, half:])
-        c_mx.append(quantize("c1", grouped1[:], SLOTS))
 
-        v_grouped = sb.tile([P, PASSES, NQ, PACK], BF16, name="v_grouped", tag="late0", align_bytes=64)
-        q_mx = []
-        for g in range(PASSES):
-            interleave(nc.scalar.copy, v_grouped[:, g, :, :], v_raw[:, g, :, :])
-            q_mx.append(quantize(f"v{g}", v_grouped[:, g, :, :], NQ))
-
-        kw_pairs = sb.tile([P, SLOTS], U32, name="kw_pairs", tag="late0", align_bytes=64)
+        kw_pairs = sb.tile([P, SLOTS], U32, name="kw_pairs", align_bytes=64)
         nc.vector.tensor_copy(out=kw_pairs[:], in_=kw_pool[:].bitcast(U32).indirect(key_list[:]))
-        kw = sb.tile([P, PASSES, 2 * SLOTS], U8, name="kw", align_bytes=64)
-        u_grouped = sb.tile([P, PASSES, NQ, PACK], BF16, name="u_grouped", tag="late1", align_bytes=64)
+        c_mx.append(quantize("c1", grouped1[:], SLOTS))
+        v1_grouped = staged("v1_grouped", [P, NQ, PACK], BF16)
+        interleave(nc.scalar.copy, v1_grouped[:], late_raw[0][:])
+        q_mx.append(quantize("v1", v1_grouped[:], NQ))
+        u_grouped = staged("u_grouped", [P, PASSES, NQ, PACK], BF16)
+        kw = staged("kw", [P, PASSES, 2 * SLOTS], U8)
         halves = kw_pairs[:].bitcast(U16).rearrange("p (n o) -> p o n", o=PASSES)
         for g in range(PASSES):
             nc.vector.tensor_copy(out=kw[:, g, :].bitcast(U16), in_=halves[:, g, :])
-            interleave(nc.scalar.copy, u_grouped[:, g, :, :], u_raw[:, g, :, :])
+            interleave(nc.scalar.copy, u_grouped[:, g, :, :], late_raw[1 + g][:])
             q_mx.append(quantize(f"u{g}", u_grouped[:, g, :, :], NQ))
 
         acc = [psum.tile([P, BANK_N], F32, name=f"acc{b}") for b in range(BANKS)]
@@ -147,7 +155,7 @@ def tile_attend_txlseg_kernel(tc, uT, vT, k_words, k_scales, cT, offs, offs2, ou
                     lhsT=q_mx[PASSES + g][0][:].bitcast(FP8X4),
                     lhsT_scale=q_mx[PASSES + g][1][:],
                     rhs=kw[:, g, 2 * b * BANK_N : 2 * (b + 1) * BANK_N].bitcast(FP4X4),
-                    rhs_scale=ks[:, g, b * BANK_N : (b + 1) * BANK_N],
+                    rhs_scale=ks[g][:, b * BANK_N : (b + 1) * BANK_N],
                     start=False,
                     stop=(g == PASSES - 1),
                 )

@@ -10,12 +10,12 @@ PASSES = D // K_PASS
 BANK_N = 128
 BANKS = SLOTS // BANK_N
 RUN = 4
+KIB = 1024
 STAGE_AT = {
-    "c4": 0, "c0": 4, "c5": 8,
-    "c6": 16, "c1": 21, "ks_both": 24, "c7": 25,
-    "v0": 33, "c2": 35, "kw_pool": 37,
-    "v1": 53, "c3": 55, "u0": 57, "u1": 61,
-    "grouped1": 66, "kw": 72, "picked1": 74, "v1_grouped": 74, "u_grouped": 78,
+    "c0": 0, "c1": 4, "c2": 8, "c3": 12, "c4": 16,
+    "c5": 0, "c6": 4, "c7": 8, "v0_raw": 12, "kw_pool": 14, "v1_raw": 0, "u0_raw": 2, "u1_raw": 4,
+    "v0_grouped": 8, "kw_pairs": 8, "u1_grouped": 8, "v1_codes": 14, "u0_codes": 15,
+    "picked1": 24, "v1_grouped": 24, "u0_grouped": 25,
 }
 
 FLOPS = 2 * 2 * D * NQ * SLOTS
@@ -44,26 +44,33 @@ def tile_attend_txlseg_kernel(tc, uT, vT, k_words, k_scales, cT, offs, offs2, ou
         stage = ctx.enter_context(tc.tile_pool(name="stage", bufs=1))
         psum = ctx.enter_context(tc.psum_pool(name="psum", bufs=1))
 
-        def staged(name, shape, dtype):
-            return stage.tile(shape, dtype, name=name, offset=STAGE_AT[name] * 512, align_bytes=64)
-
         c_rows = cT.rearrange("(g p t) n -> g t p n", p=P, t=PACK)
         c_pool = {}
+
+        def staged(name, shape, dtype):
+            if name not in STAGE_AT:
+                return sb.tile(shape, dtype, name=name, align_bytes=64)
+            return stage.tile(shape, dtype, name=name, offset=STAGE_AT[name] * KIB, align_bytes=64)
 
         def load_plane(j):
             c_pool[j] = staged(f"c{j}", [P, C], F32)
             nc.sync.dma_start(out=c_pool[j][:], in_=c_rows[j // PACK, j % PACK])
 
         def load_queries(name, queries, g):
-            raw = staged(f"{name}{g}", [P, PACK, NQ], F32)
+            raw = staged(f"{name}{g}_raw", [P, PACK, NQ], F32)
             nc.sync.dma_start(out=raw[:], in_=queries[0].rearrange("(g p t) q -> g p t q", p=P, t=PACK)[g])
             return raw
 
         def quantize(name, grouped, width):
-            codes = sb.tile([P, width], U32, name=f"{name}_codes", align_bytes=64)
-            scales = sb.tile([P, width], U8, name=f"{name}_scales", align_bytes=64)
+            codes = staged(f"{name}_codes", [P, width], U32)
+            scales = staged(f"{name}_scales", [P, width], U8)
             nc.vector.quantize_mx(out=codes[:].bitcast(FP8X4), scales=scales[:], in_=grouped.rearrange("p n t -> p (n t)"))
             return codes, scales
+
+        def quantize_queries(name, raw, copy):
+            grouped = staged(f"{name}_grouped", [P, NQ, PACK], BF16)
+            interleave(copy, grouped[:], raw[:])
+            return quantize(name, grouped[:], NQ)
 
         def gather_plane(picked, j, s0, s1):
             nc.vector.tensor_copy(
@@ -76,89 +83,77 @@ def tile_attend_txlseg_kernel(tc, uT, vT, k_words, k_scales, cT, offs, offs2, ou
         ks_second = sb.tile([P, SLOTS // 4], I32, name="ks_second", align_bytes=64)
         nc.vector.memset(ks_pool[:], 0)
         nc.vector.memset(ks_second[:], 0)
+        scale_rows = k_scales.rearrange("o (q r) t -> r q o t", r=4)
         load_plane(0)
         nc.sync.dma_start(pos_list[:], offs2)
-        load_plane(1)
-        scale_rows = k_scales.rearrange("o (q r) t -> r q o t", r=4)
+        for j in (1, 2, 3):
+            load_plane(j)
+        nc.sync.dma_start(key_list[:], offs)
+        load_plane(4)
         for r in range(4):
             nc.sync.dma_start(out=ks_pool[r:P:16, :], in_=scale_rows[r].bitcast(I32))
-        load_plane(2)
-        nc.sync.dma_start(key_list[:], offs)
-        load_plane(3)
 
-        picked0 = sb.tile([P, PACK, SLOTS], F32, name="picked0", tag="picked0", align_bytes=64)
+        picked0 = staged("picked0", [P, PACK, SLOTS], F32)
         picked1 = staged("picked1", [P, PACK, SLOTS], F32)
-        grouped0 = sb.tile([P, SLOTS, PACK], BF16, name="grouped0", align_bytes=64)
+        grouped0 = staged("grouped0", [P, SLOTS, PACK], BF16)
         grouped1 = staged("grouped1", [P, SLOTS, PACK], BF16)
         half = SLOTS // 2
-        gather_plane(picked0, 0, 0, SLOTS)
-        load_plane(4)
-        load_plane(5)
-        gather_plane(picked0, 1, 0, SLOTS)
-        load_plane(6)
-        load_plane(7)
+        for j in range(3):
+            gather_plane(picked0, j, 0, SLOTS)
+            load_plane(5 + j)
+        gather_plane(picked0, 3, 0, SLOTS)
+        v0_raw = load_queries("v", vT, 0)
+        interleave(nc.scalar.copy, grouped0[:], picked0[:])
+        gather_plane(picked1, 4, 0, SLOTS)
+        kw_pool = staged("kw_pool", [P, T], I32)
+        nc.sync.dma_start(out=kw_pool[:], in_=k_words[0].rearrange("p t b -> p (t b)").bitcast(I32))
         ks_both = staged("ks_both", [P, SLOTS], U8)
         nc.vector.tensor_copy(out=ks_both[:], in_=ks_pool[:].bitcast(U8).indirect(key_list[:]))
         nc.sync.dma_start(out=ks_second[0 : P - 16, :], in_=ks_both[16:P, :].bitcast(I32))
         ks = [ks_both[:], ks_second[:].bitcast(U8)]
-        gather_plane(picked0, 2, 0, SLOTS)
-        v0_raw = load_queries("v", vT, 0)
-        kw_pool = staged("kw_pool", [P, T], I32)
-        nc.sync.dma_start(out=kw_pool[:], in_=k_words[0].rearrange("p t b -> p (t b)").bitcast(I32))
-        gather_plane(picked0, 3, 0, SLOTS)
-        late_raw = [load_queries("v", vT, 1), load_queries("u", uT, 0), load_queries("u", uT, 1)]
-        interleave(nc.scalar.copy, grouped0[:], picked0[:])
-        for j in (4, 5, 6):
-            gather_plane(picked1, j, 0, SLOTS)
+        gather_plane(picked1, 5, 0, SLOTS)
+        v1_raw = load_queries("v", vT, 1)
+        u0_raw = load_queries("u", uT, 0)
         c_mx = [quantize("c0", grouped0[:], SLOTS)]
-        v0_grouped = sb.tile([P, NQ, PACK], BF16, name="v0_grouped", tag="picked0", align_bytes=64)
-        interleave(nc.scalar.copy, v0_grouped[:], v0_raw[:])
-        gather_plane(picked1, 7, 0, half)
-        interleave(nc.scalar.copy, grouped1[:, :half, :], picked1[:, :, :half])
-        gather_plane(picked1, 7, half, SLOTS)
-        q_mx = [quantize("v0", v0_grouped[:], NQ)]
-        interleave(nc.vector.tensor_copy, grouped1[:, half:, :], picked1[:, :, half:])
-
-        kw_pairs = sb.tile([P, SLOTS], U32, name="kw_pairs", align_bytes=64)
-        nc.vector.tensor_copy(out=kw_pairs[:], in_=kw_pool[:].bitcast(U32).indirect(key_list[:]))
+        gather_plane(picked1, 6, 0, SLOTS)
+        u1_raw = load_queries("u", uT, 1)
+        for s0, copy in ((0, nc.scalar.copy), (half, nc.vector.tensor_copy)):
+            gather_plane(picked1, 7, s0, s0 + half)
+            interleave(copy, grouped1[:, s0 : s0 + half, :], picked1[:, :, s0 : s0 + half])
         c_mx.append(quantize("c1", grouped1[:], SLOTS))
-        v1_grouped = staged("v1_grouped", [P, NQ, PACK], BF16)
-        interleave(nc.scalar.copy, v1_grouped[:], late_raw[0][:])
-        q_mx.append(quantize("v1", v1_grouped[:], NQ))
-        u_grouped = staged("u_grouped", [P, PASSES, NQ, PACK], BF16)
+        v_mx = [quantize_queries("v0", v0_raw, nc.scalar.copy)]
+
+        kw_pairs = staged("kw_pairs", [P, SLOTS], U32)
+        nc.vector.tensor_copy(out=kw_pairs[:], in_=kw_pool[:].bitcast(U32).indirect(key_list[:]))
         kw = staged("kw", [P, PASSES, 2 * SLOTS], U8)
-        halves = kw_pairs[:].bitcast(U16).rearrange("p (n o) -> p o n", o=PASSES)
-        for g in range(PASSES):
-            nc.vector.tensor_copy(out=kw[:, g, :].bitcast(U16), in_=halves[:, g, :])
-            interleave(nc.scalar.copy, u_grouped[:, g, :, :], late_raw[1 + g][:])
-            q_mx.append(quantize(f"u{g}", u_grouped[:, g, :, :], NQ))
+        nc.vector.tensor_copy(
+            out=kw[:].bitcast(U16), in_=kw_pairs[:].bitcast(U16).rearrange("p (n o) -> p o n", o=PASSES)
+        )
+        v_mx.append(quantize_queries("v1", v1_raw, nc.scalar.copy))
+        u_mx = [quantize_queries("u0", u0_raw, nc.scalar.copy), quantize_queries("u1", u1_raw, nc.vector.tensor_copy)]
+
+        def position_pass(g):
+            return (v_mx[g][0][:], v_mx[g][1][:]), lambda a, b: (c_mx[g][0][:, a:b].bitcast(FP8X4), c_mx[g][1][:, a:b])
+
+        def content_pass(g):
+            return (u_mx[g][0][:], u_mx[g][1][:]), lambda a, b: (kw[:, g, 2 * a : 2 * b].bitcast(FP4X4), ks[g][:, a:b])
 
         acc = [psum.tile([P, BANK_N], F32, name=f"acc{b}") for b in range(BANKS)]
-        for g in range(PASSES):
+        passes = [position_pass(0), position_pass(1), content_pass(0), content_pass(1)]
+        for i, (rows, moving) in enumerate(passes):
             for b in range(BANKS):
-                cols = slice(b * BANK_N, (b + 1) * BANK_N)
+                codes, scales = moving(b * BANK_N, (b + 1) * BANK_N)
                 nc.tensor.matmul_mx(
                     out=acc[b][:],
-                    lhsT=q_mx[g][0][:].bitcast(FP8X4),
-                    lhsT_scale=q_mx[g][1][:],
-                    rhs=c_mx[g][0][:, cols].bitcast(FP8X4),
-                    rhs_scale=c_mx[g][1][:, cols],
-                    start=(g == 0),
-                    stop=False,
+                    lhsT=rows[0].bitcast(FP8X4),
+                    lhsT_scale=rows[1],
+                    rhs=codes,
+                    rhs_scale=scales,
+                    start=(i == 0),
+                    stop=(i == len(passes) - 1),
                 )
         best = sb.tile([P, SLOTS // SEG], F32, name="best")
         pages = BANK_N // SEG
-        for g in range(PASSES):
-            for b in range(BANKS):
-                nc.tensor.matmul_mx(
-                    out=acc[b][:],
-                    lhsT=q_mx[PASSES + g][0][:].bitcast(FP8X4),
-                    lhsT_scale=q_mx[PASSES + g][1][:],
-                    rhs=kw[:, g, 2 * b * BANK_N : 2 * (b + 1) * BANK_N].bitcast(FP4X4),
-                    rhs_scale=ks[g][:, b * BANK_N : (b + 1) * BANK_N],
-                    start=False,
-                    stop=(g == PASSES - 1),
-                )
         for b in range(BANKS):
             nc.vector.tensor_reduce(
                 out=best[:, b * pages : (b + 1) * pages],

@@ -13,9 +13,9 @@ RUN = 4
 KIB = 1024
 STAGE_AT = {
     "c0": 0, "c1": 4, "c2": 8, "c3": 12, "c4": 16,
-    "c5": 0, "c6": 4, "c7": 8, "v0_raw": 12, "kw_pool": 14, "v1_raw": 0, "u0_raw": 2, "u1_raw": 4,
-    "v0_grouped": 8, "kw_pairs": 8, "u1_grouped": 8, "v1_codes": 14, "u0_codes": 15,
-    "picked1": 24, "v1_grouped": 24, "u0_grouped": 25,
+    "c5": 0, "c6": 4, "c7": 8, "v0_raw": 12, "ks_both": 16, "kw_pool": 17, "v1_raw": 0, "u0_raw": 2, "u1_raw": 4,
+    "v0_grouped": 8, "kw_pairs": 8, "u1_grouped": 8, "v1_codes": 17, "u0_codes": 18,
+    "picked1": 28, "v1_grouped": 28, "u0_grouped": 29,
 }
 
 FLOPS = 2 * 2 * D * NQ * SLOTS
@@ -91,7 +91,7 @@ def tile_attend_txlseg_kernel(tc, uT, vT, k_words, k_scales, cT, offs, offs2, ou
         nc.sync.dma_start(key_list[:], offs)
         load_plane(4)
         for r in range(4):
-            nc.sync.dma_start(out=ks_pool[r:P:16, :], in_=scale_rows[r].bitcast(I32))
+            nc.gpsimd.dma_start(out=ks_pool[r:P:16, :], in_=scale_rows[r].bitcast(I32))
 
         picked0 = staged("picked0", [P, PACK, SLOTS], F32)
         picked1 = staged("picked1", [P, PACK, SLOTS], F32)

@@ -10,11 +10,12 @@ PASSES = D // K_PASS
 BANK_N = 128
 BANKS = SLOTS // BANK_N
 RUN = 4
+LAST_ROWS_ON_VECTOR = 48
 KIB = 1024
 STAGE_AT = {
     "c0": 0, "c1": 4, "c2": 8, "c3": 12, "c4": 16,
     "c5": 0, "c6": 4, "c7": 8, "v0_raw": 12, "ks_both": 16, "kw_pool": 17, "v1_raw": 0, "u0_raw": 2, "u1_raw": 4,
-    "v0_grouped": 8, "kw_pairs": 8, "u1_grouped": 8, "v1_codes": 17, "u0_codes": 18,
+    "v0_grouped": 8, "kw_pairs": 8, "u1_grouped": 8, "v1_codes": 17, "u0_codes": 18, "kw": 0,
     "picked1": 28, "v1_grouped": 28, "u0_grouped": 29,
 }
 
@@ -109,7 +110,8 @@ def tile_attend_txlseg_kernel(tc, uT, vT, k_words, k_scales, cT, offs, offs2, ou
         nc.sync.dma_start(out=kw_pool[:], in_=k_words[0].rearrange("p t b -> p (t b)").bitcast(I32))
         ks_both = staged("ks_both", [P, SLOTS], U8)
         nc.vector.tensor_copy(out=ks_both[:], in_=ks_pool[:].bitcast(U8).indirect(key_list[:]))
-        nc.sync.dma_start(out=ks_second[0 : P - 16, :], in_=ks_both[16:P, :].bitcast(I32))
+        for r in range(4):
+            nc.gpsimd.dma_start(out=ks_second[r:P:32, :], in_=ks_both[16 + r : P : 32, :].bitcast(I32))
         ks = [ks_both[:], ks_second[:].bitcast(U8)]
         gather_plane(picked1, 5, 0, SLOTS)
         v1_raw = load_queries("v", vT, 1)
@@ -125,12 +127,17 @@ def tile_attend_txlseg_kernel(tc, uT, vT, k_words, k_scales, cT, offs, offs2, ou
 
         kw_pairs = staged("kw_pairs", [P, SLOTS], U32)
         nc.vector.tensor_copy(out=kw_pairs[:], in_=kw_pool[:].bitcast(U32).indirect(key_list[:]))
+        v_mx.append(quantize_queries("v1", v1_raw, nc.scalar.copy))
         kw = staged("kw", [P, PASSES, 2 * SLOTS], U8)
         nc.vector.tensor_copy(
             out=kw[:].bitcast(U16), in_=kw_pairs[:].bitcast(U16).rearrange("p (n o) -> p o n", o=PASSES)
         )
-        v_mx.append(quantize_queries("v1", v1_raw, nc.scalar.copy))
-        u_mx = [quantize_queries("u0", u0_raw, nc.scalar.copy), quantize_queries("u1", u1_raw, nc.vector.tensor_copy)]
+        u_mx = [quantize_queries("u0", u0_raw, nc.scalar.copy)]
+        u1_grouped = staged("u1_grouped", [P, NQ, PACK], BF16)
+        cut = LAST_ROWS_ON_VECTOR
+        interleave(nc.scalar.copy, u1_grouped[:, cut:, :], u1_raw[:, :, cut:])
+        interleave(nc.vector.tensor_copy, u1_grouped[:, :cut, :], u1_raw[:, :, :cut])
+        u_mx.append(quantize("u1", u1_grouped[:], NQ))
 
         def position_pass(g):
             return (v_mx[g][0][:], v_mx[g][1][:]), lambda a, b: (c_mx[g][0][:, a:b].bitcast(FP8X4), c_mx[g][1][:, a:b])

@@ -10,13 +10,14 @@ PASSES = D // K_PASS
 BANK_N = 128
 BANKS = SLOTS // BANK_N
 RUN = 4
-LAST_ROWS_ON_VECTOR = 48
 KIB = 1024
 STAGE_AT = {
     "c0": 0, "c1": 4, "c2": 8, "c3": 12, "c4": 16,
-    "c5": 0, "c6": 4, "c7": 8, "v0_raw": 12, "ks_both": 16, "kw_pool": 17, "v1_raw": 0, "u0_raw": 2, "u1_raw": 4,
-    "v0_grouped": 8, "kw_pairs": 8, "u1_grouped": 8, "v1_codes": 17, "u0_codes": 18, "kw": 0,
-    "picked1": 28, "v1_grouped": 28, "u0_grouped": 29,
+    "c5": 0, "c6": 4, "v0_raw": 8, "c7": 12, "ks_both": 16, "kw_pool": 17,
+    "v1_raw": 0, "v0_codes": 2, "u0_raw": 4, "u1_raw": 6,
+    "v1_codes": 17, "u0_codes": 18, "kw0": 0, "kw1": 4,
+    "picked1": 28, "v1_grouped": 28, "u0_grouped": 29, "u1_grouped": 30, "c1b_codes": 31,
+    "grouped1a": 36, "kw_pairs": 36,
 }
 
 FLOPS = 2 * 2 * D * NQ * SLOTS
@@ -97,53 +98,65 @@ def tile_attend_txlseg_kernel(tc, uT, vT, k_words, k_scales, cT, offs, offs2, ou
         picked0 = staged("picked0", [P, PACK, SLOTS], F32)
         picked1 = staged("picked1", [P, PACK, SLOTS], F32)
         grouped0 = staged("grouped0", [P, SLOTS, PACK], BF16)
-        grouped1 = staged("grouped1", [P, SLOTS, PACK], BF16)
-        half = SLOTS // 2
-        for j in range(3):
+        half, quarter = SLOTS // 2, SLOTS // 4
+        for j in range(2):
             gather_plane(picked0, j, 0, SLOTS)
             load_plane(5 + j)
-        gather_plane(picked0, 3, 0, SLOTS)
+        gather_plane(picked0, 2, 0, SLOTS)
         v0_raw = load_queries("v", vT, 0)
+        gather_plane(picked0, 3, 0, SLOTS)
+        load_plane(7)
         interleave(nc.scalar.copy, grouped0[:], picked0[:])
         gather_plane(picked1, 4, 0, SLOTS)
         kw_pool = staged("kw_pool", [P, T], I32)
         nc.sync.dma_start(out=kw_pool[:], in_=k_words[0].rearrange("p t b -> p (t b)").bitcast(I32))
         ks_both = staged("ks_both", [P, SLOTS], U8)
         nc.vector.tensor_copy(out=ks_both[:], in_=ks_pool[:].bitcast(U8).indirect(key_list[:]))
-        for r in range(4):
-            nc.gpsimd.dma_start(out=ks_second[r:P:32, :], in_=ks_both[16 + r : P : 32, :].bitcast(I32))
+        nc.sync.dma_start(out=ks_second[0 : P - 16, :], in_=ks_both[16:P, :].bitcast(I32))
         ks = [ks_both[:], ks_second[:].bitcast(U8)]
         gather_plane(picked1, 5, 0, SLOTS)
         v1_raw = load_queries("v", vT, 1)
-        u0_raw = load_queries("u", uT, 0)
-        c_mx = [quantize("c0", grouped0[:], SLOTS)]
+        c0_mx = quantize("c0", grouped0[:], SLOTS)
         gather_plane(picked1, 6, 0, SLOTS)
+        u0_raw = load_queries("u", uT, 0)
         u1_raw = load_queries("u", uT, 1)
-        for s0, copy in ((0, nc.scalar.copy), (half, nc.vector.tensor_copy)):
-            gather_plane(picked1, 7, s0, s0 + half)
-            interleave(copy, grouped1[:, s0 : s0 + half, :], picked1[:, :, s0 : s0 + half])
-        c_mx.append(quantize("c1", grouped1[:], SLOTS))
         v_mx = [quantize_queries("v0", v0_raw, nc.scalar.copy)]
+        grouped1a = staged("grouped1a", [P, half, PACK], BF16)
+        grouped1b = staged("grouped1b", [P, half, PACK], BF16)
+        gather_plane(picked1, 7, 0, half)
+        interleave(nc.scalar.copy, grouped1a[:], picked1[:, :, :half])
+        for s0 in (half, half + quarter):
+            gather_plane(picked1, 7, s0, s0 + quarter)
+        for s0 in (0, quarter):
+            interleave(
+                nc.vector.tensor_copy, grouped1b[:, s0 : s0 + quarter, :], picked1[:, :, half + s0 : half + s0 + quarter]
+            )
+        c1_mx = [quantize("c1a", grouped1a[:], half), quantize("c1b", grouped1b[:], half)]
 
         kw_pairs = staged("kw_pairs", [P, SLOTS], U32)
         nc.vector.tensor_copy(out=kw_pairs[:], in_=kw_pool[:].bitcast(U32).indirect(key_list[:]))
         v_mx.append(quantize_queries("v1", v1_raw, nc.scalar.copy))
-        kw = staged("kw", [P, PASSES, 2 * SLOTS], U8)
-        nc.vector.tensor_copy(
-            out=kw[:].bitcast(U16), in_=kw_pairs[:].bitcast(U16).rearrange("p (n o) -> p o n", o=PASSES)
-        )
-        u_mx = [quantize_queries("u0", u0_raw, nc.scalar.copy)]
-        u1_grouped = staged("u1_grouped", [P, NQ, PACK], BF16)
-        cut = LAST_ROWS_ON_VECTOR
-        interleave(nc.scalar.copy, u1_grouped[:, cut:, :], u1_raw[:, :, cut:])
-        interleave(nc.vector.tensor_copy, u1_grouped[:, :cut, :], u1_raw[:, :, :cut])
-        u_mx.append(quantize("u1", u1_grouped[:], NQ))
+        halves = kw_pairs[:].bitcast(U16).rearrange("p (n o) -> p o n", o=PASSES)
+        kw, u_mx = [], []
+        for g, raw in enumerate((u0_raw, u1_raw)):
+            kw.append(staged(f"kw{g}", [P, 2 * SLOTS], U8))
+            grouped = staged(f"u{g}_grouped", [P, NQ, PACK], BF16)
+            interleave(nc.scalar.copy, grouped[:], raw[:])
+            nc.vector.tensor_copy(out=kw[g][:].bitcast(U16), in_=halves[:, g, :])
+            u_mx.append(quantize(f"u{g}", grouped[:], NQ))
+
+        def first_positions(a, b):
+            return c0_mx[0][:, a:b].bitcast(FP8X4), c0_mx[1][:, a:b]
+
+        def second_positions(a, b):
+            codes, scales = c1_mx[a // half]
+            return codes[:, a % half : a % half + b - a].bitcast(FP8X4), scales[:, a % half : a % half + b - a]
 
         def position_pass(g):
-            return (v_mx[g][0][:], v_mx[g][1][:]), lambda a, b: (c_mx[g][0][:, a:b].bitcast(FP8X4), c_mx[g][1][:, a:b])
+            return (v_mx[g][0][:], v_mx[g][1][:]), (first_positions, second_positions)[g]
 
         def content_pass(g):
-            return (u_mx[g][0][:], u_mx[g][1][:]), lambda a, b: (kw[:, g, 2 * a : 2 * b].bitcast(FP4X4), ks[g][:, a:b])
+            return (u_mx[g][0][:], u_mx[g][1][:]), lambda a, b: (kw[g][:, 2 * a : 2 * b].bitcast(FP4X4), ks[g][:, a:b])
 
         acc = [psum.tile([P, BANK_N], F32, name=f"acc{b}") for b in range(BANKS)]
         passes = [position_pass(0), position_pass(1), content_pass(0), content_pass(1)]

@@ -10,13 +10,14 @@ PASSES = D // K_PASS
 BANK_N = 128
 BANKS = SLOTS // BANK_N
 RUN = 4
+LAST_ROWS_ON_VECTOR = 64
 KIB = 1024
 STAGE_AT = {
     "c0": 0, "c1": 4, "c2": 8, "c3": 12, "c4": 16,
     "c5": 0, "c6": 4, "v0_raw": 8, "c7": 12, "ks_both": 16, "kw_pool": 17,
     "v1_raw": 0, "v0_codes": 2, "u0_raw": 4, "u1_raw": 6,
     "v1_codes": 17, "u0_codes": 18, "kw0": 0, "kw1": 4,
-    "picked1": 28, "v1_grouped": 28, "u0_grouped": 29, "u1_grouped": 30, "c1b_codes": 31,
+    "picked1": 28, "v1_grouped": 28, "u0_grouped": 29, "u1_grouped": 28, "c1b_codes": 31,
     "grouped1a": 36, "kw_pairs": 36,
 }
 
@@ -112,7 +113,8 @@ def tile_attend_txlseg_kernel(tc, uT, vT, k_words, k_scales, cT, offs, offs2, ou
         nc.sync.dma_start(out=kw_pool[:], in_=k_words[0].rearrange("p t b -> p (t b)").bitcast(I32))
         ks_both = staged("ks_both", [P, SLOTS], U8)
         nc.vector.tensor_copy(out=ks_both[:], in_=ks_pool[:].bitcast(U8).indirect(key_list[:]))
-        nc.sync.dma_start(out=ks_second[0 : P - 16, :], in_=ks_both[16:P, :].bitcast(I32))
+        for r in range(4):
+            nc.gpsimd.dma_start(out=ks_second[r:P:32, :], in_=ks_both[16 + r : P : 32, :].bitcast(I32))
         ks = [ks_both[:], ks_second[:].bitcast(U8)]
         gather_plane(picked1, 5, 0, SLOTS)
         v1_raw = load_queries("v", vT, 1)
@@ -141,7 +143,10 @@ def tile_attend_txlseg_kernel(tc, uT, vT, k_words, k_scales, cT, offs, offs2, ou
         for g, raw in enumerate((u0_raw, u1_raw)):
             kw.append(staged(f"kw{g}", [P, 2 * SLOTS], U8))
             grouped = staged(f"u{g}_grouped", [P, NQ, PACK], BF16)
-            interleave(nc.scalar.copy, grouped[:], raw[:])
+            cut = LAST_ROWS_ON_VECTOR * g
+            interleave(nc.scalar.copy, grouped[:, cut:, :], raw[:, :, cut:])
+            if cut:
+                interleave(nc.vector.tensor_copy, grouped[:, :cut, :], raw[:, :, :cut])
             nc.vector.tensor_copy(out=kw[g][:].bitcast(U16), in_=halves[:, g, :])
             u_mx.append(quantize(f"u{g}", grouped[:], NQ))
 

@@ -9,16 +9,15 @@ D, T, C, NQ, SLOTS, SEG = 1024, 2048, 1024, 128, 512, 32
 PASSES = D // K_PASS
 BANK_N = 128
 BANKS = SLOTS // BANK_N
+HALF = SLOTS // 2
 RUN = 4
-LAST_ROWS_ON_VECTOR = 64
+ROWS_ON_VECTOR = 64
+PLANE_LOADS = ((0, 2), (2, 4), (4, 6), (6, 7), (7, 8))
 KIB = 1024
 STAGE_AT = {
-    "c0": 0, "c1": 4, "c2": 8, "c3": 12, "c4": 16,
-    "c5": 0, "c6": 4, "v0_raw": 8, "c7": 12, "ks_both": 16, "kw_pool": 17,
-    "v1_raw": 0, "v0_codes": 2, "u0_raw": 4, "u1_raw": 6,
-    "v1_codes": 17, "u0_codes": 18, "kw0": 0, "kw1": 4,
-    "picked1": 28, "v1_grouped": 28, "u0_grouped": 29, "u1_grouped": 28, "c1b_codes": 31,
-    "grouped1a": 36, "kw_pairs": 36,
+    "c0": 0, "ks_both": 0,
+    "ks_pool": 8, "picked1": 8, "v0_grouped": 10, "v1_grouped": 11, "kw_pairs0": 12, "kw_pairs1": 13, "u0_grouped": 13,
+    "u0_raw": 16, "u1_grouped": 16,
 }
 
 FLOPS = 2 * 2 * D * NQ * SLOTS
@@ -47,17 +46,20 @@ def tile_attend_txlseg_kernel(tc, uT, vT, k_words, k_scales, cT, offs, offs2, ou
         stage = ctx.enter_context(tc.tile_pool(name="stage", bufs=1))
         psum = ctx.enter_context(tc.psum_pool(name="psum", bufs=1))
 
-        c_rows = cT.rearrange("(g p t) n -> g t p n", p=P, t=PACK)
-        c_pool = {}
-
         def staged(name, shape, dtype):
             if name not in STAGE_AT:
                 return sb.tile(shape, dtype, name=name, align_bytes=64)
             return stage.tile(shape, dtype, name=name, offset=STAGE_AT[name] * KIB, align_bytes=64)
 
-        def load_plane(j):
-            c_pool[j] = staged(f"c{j}", [P, C], F32)
-            nc.sync.dma_start(out=c_pool[j][:], in_=c_rows[j // PACK, j % PACK])
+        c_rows = cT.rearrange("(g p t) n -> g p t n", p=P, t=PACK)
+        windows = {}
+
+        def load_planes(j0, j1):
+            planes = staged(f"c{j0}", [P, j1 - j0, C], F32)
+            g, t = divmod(j0, PACK)
+            nc.sync.dma_start(out=planes[:], in_=c_rows[g, :, t : t + j1 - j0, :])
+            for j in range(j0, j1):
+                windows[j] = planes[:, j - j0, :]
 
         def load_queries(name, queries, g):
             raw = staged(f"{name}{g}_raw", [P, PACK, NQ], F32)
@@ -70,108 +72,99 @@ def tile_attend_txlseg_kernel(tc, uT, vT, k_words, k_scales, cT, offs, offs2, ou
             nc.vector.quantize_mx(out=codes[:].bitcast(FP8X4), scales=scales[:], in_=grouped.rearrange("p n t -> p (n t)"))
             return codes, scales
 
-        def quantize_queries(name, raw, copy):
-            grouped = staged(f"{name}_grouped", [P, NQ, PACK], BF16)
-            interleave(copy, grouped[:], raw[:])
-            return quantize(name, grouped[:], NQ)
-
         def gather_plane(picked, j, s0, s1):
             nc.vector.tensor_copy(
-                out=picked[:, j % PACK, s0:s1], in_=c_pool[j][:].indirect(pos_list[:, s0 // 16 : s1 // 16])
+                out=picked[:, j % PACK, s0:s1], in_=windows[j].indirect(pos_list[:, s0 // 16 : s1 // 16])
             )
+
+        def group_positions(g, picked):
+            gather_plane(picked, PACK * g + 3, 0, HALF)
+            first = staged(f"grouped{g}a", [P, HALF, PACK], BF16)
+            interleave(nc.scalar.copy, first[:], picked[:, :, :HALF])
+            gather_plane(picked, PACK * g + 3, HALF, SLOTS)
+            second = staged(f"grouped{g}b", [P, HALF, PACK], BF16)
+            interleave(nc.vector.tensor_copy, second[:], picked[:, :, HALF:])
+            return first, second
+
+        def group_queries(name, raw, cut):
+            grouped = staged(f"{name}_grouped", [P, NQ, PACK], BF16)
+            interleave(nc.scalar.copy, grouped[:, cut:, :], raw[:, :, cut:])
+            if cut:
+                interleave(nc.vector.tensor_copy, grouped[:, :cut, :], raw[:, :, :cut])
+            return grouped
 
         key_list = sb.tile([P, SLOTS // 16], U16, name="key_list")
         pos_list = sb.tile([P, SLOTS // 16], U16, name="pos_list")
-        ks_pool = sb.tile([P, T // 4], I32, name="ks_pool", align_bytes=64)
-        ks_second = sb.tile([P, SLOTS // 4], I32, name="ks_second", align_bytes=64)
+        ks_pool = staged("ks_pool", [P, T // 4], I32)
+        ks_second = staged("ks_second", [P, SLOTS // 4], I32)
         nc.vector.memset(ks_pool[:], 0)
         nc.vector.memset(ks_second[:], 0)
-        scale_rows = k_scales.rearrange("o (q r) t -> r q o t", r=4)
-        load_plane(0)
+        load_planes(*PLANE_LOADS[0])
         nc.sync.dma_start(pos_list[:], offs2)
-        for j in (1, 2, 3):
-            load_plane(j)
         nc.sync.dma_start(key_list[:], offs)
-        load_plane(4)
+        for span in PLANE_LOADS[1:]:
+            load_planes(*span)
+        kw_pool = staged("kw_pool", [P, T], I32)
+        nc.sync.dma_start(out=kw_pool[:], in_=k_words[0].rearrange("p t b -> p (t b)").bitcast(I32))
+        v_raw = [load_queries("v", vT, g) for g in range(PASSES)]
+        u_raw = [load_queries("u", uT, g) for g in range(PASSES)]
+        scale_rows = k_scales.rearrange("o (q r) t -> r q o t", r=4)
         for r in range(4):
             nc.gpsimd.dma_start(out=ks_pool[r:P:16, :], in_=scale_rows[r].bitcast(I32))
 
         picked0 = staged("picked0", [P, PACK, SLOTS], F32)
-        picked1 = staged("picked1", [P, PACK, SLOTS], F32)
-        grouped0 = staged("grouped0", [P, SLOTS, PACK], BF16)
-        half, quarter = SLOTS // 2, SLOTS // 4
-        for j in range(2):
+        for j in (0, 1):
             gather_plane(picked0, j, 0, SLOTS)
-            load_plane(5 + j)
-        gather_plane(picked0, 2, 0, SLOTS)
-        v0_raw = load_queries("v", vT, 0)
-        gather_plane(picked0, 3, 0, SLOTS)
-        load_plane(7)
-        interleave(nc.scalar.copy, grouped0[:], picked0[:])
-        gather_plane(picked1, 4, 0, SLOTS)
-        kw_pool = staged("kw_pool", [P, T], I32)
-        nc.sync.dma_start(out=kw_pool[:], in_=k_words[0].rearrange("p t b -> p (t b)").bitcast(I32))
         ks_both = staged("ks_both", [P, SLOTS], U8)
         nc.vector.tensor_copy(out=ks_both[:], in_=ks_pool[:].bitcast(U8).indirect(key_list[:]))
         for r in range(4):
             nc.gpsimd.dma_start(out=ks_second[r:P:32, :], in_=ks_both[16 + r : P : 32, :].bitcast(I32))
         ks = [ks_both[:], ks_second[:].bitcast(U8)]
-        gather_plane(picked1, 5, 0, SLOTS)
-        v1_raw = load_queries("v", vT, 1)
-        c0_mx = quantize("c0", grouped0[:], SLOTS)
+        gather_plane(picked0, 2, 0, SLOTS)
+        grouped0 = group_positions(0, picked0)
+        picked1 = staged("picked1", [P, PACK, SLOTS], F32)
+        for j in (4, 5):
+            gather_plane(picked1, j, 0, SLOTS)
+        c_mx = [[quantize(f"c0{h}", grouped0[h][:], HALF) for h in range(2)]]
         gather_plane(picked1, 6, 0, SLOTS)
-        u0_raw = load_queries("u", uT, 0)
-        u1_raw = load_queries("u", uT, 1)
-        v_mx = [quantize_queries("v0", v0_raw, nc.scalar.copy)]
-        grouped1a = staged("grouped1a", [P, half, PACK], BF16)
-        grouped1b = staged("grouped1b", [P, half, PACK], BF16)
-        gather_plane(picked1, 7, 0, half)
-        interleave(nc.scalar.copy, grouped1a[:], picked1[:, :, :half])
-        for s0 in (half, half + quarter):
-            gather_plane(picked1, 7, s0, s0 + quarter)
-        for s0 in (0, quarter):
-            interleave(
-                nc.vector.tensor_copy, grouped1b[:, s0 : s0 + quarter, :], picked1[:, :, half + s0 : half + s0 + quarter]
+        grouped1 = group_positions(1, picked1)
+        c_mx.append([quantize(f"c1{h}", grouped1[h][:], HALF) for h in range(2)])
+
+        kw_pairs = [staged(f"kw_pairs{h}", [P, HALF], U32) for h in range(2)]
+        for h in range(2):
+            nc.vector.tensor_copy(
+                out=kw_pairs[h][:], in_=kw_pool[:].bitcast(U32).indirect(key_list[:, h * HALF // 16 : (h + 1) * HALF // 16])
             )
-        c1_mx = [quantize("c1a", grouped1a[:], half), quantize("c1b", grouped1b[:], half)]
+        kw = [staged(f"kw{h}", [P, PASSES, 2 * HALF], U8) for h in range(2)]
+        for h in range(2):
+            nc.vector.tensor_copy(
+                out=kw[h][:].bitcast(U16), in_=kw_pairs[h][:].bitcast(U16).rearrange("p (n o) -> p o n", o=PASSES)
+            )
+        v_mx = [quantize("v0", group_queries("v0", v_raw[0], 0)[:], NQ)]
+        v1_grouped = group_queries("v1", v_raw[1], 0)
+        u0_grouped = group_queries("u0", u_raw[0], ROWS_ON_VECTOR)
+        v_mx.append(quantize("v1", v1_grouped[:], NQ))
+        u_mx = [quantize("u0", u0_grouped[:], NQ)]
+        u_mx.append(quantize("u1", group_queries("u1", u_raw[1], ROWS_ON_VECTOR)[:], NQ))
 
-        kw_pairs = staged("kw_pairs", [P, SLOTS], U32)
-        nc.vector.tensor_copy(out=kw_pairs[:], in_=kw_pool[:].bitcast(U32).indirect(key_list[:]))
-        v_mx.append(quantize_queries("v1", v1_raw, nc.scalar.copy))
-        halves = kw_pairs[:].bitcast(U16).rearrange("p (n o) -> p o n", o=PASSES)
-        kw, u_mx = [], []
-        for g, raw in enumerate((u0_raw, u1_raw)):
-            kw.append(staged(f"kw{g}", [P, 2 * SLOTS], U8))
-            grouped = staged(f"u{g}_grouped", [P, NQ, PACK], BF16)
-            cut = LAST_ROWS_ON_VECTOR * g
-            interleave(nc.scalar.copy, grouped[:, cut:, :], raw[:, :, cut:])
-            if cut:
-                interleave(nc.vector.tensor_copy, grouped[:, :cut, :], raw[:, :, :cut])
-            nc.vector.tensor_copy(out=kw[g][:].bitcast(U16), in_=halves[:, g, :])
-            u_mx.append(quantize(f"u{g}", grouped[:], NQ))
+        def positions(g, b):
+            h, a = divmod(b * BANK_N, HALF)
+            codes, scales = c_mx[g][h]
+            return codes[:, a : a + BANK_N].bitcast(FP8X4), scales[:, a : a + BANK_N]
 
-        def first_positions(a, b):
-            return c0_mx[0][:, a:b].bitcast(FP8X4), c0_mx[1][:, a:b]
-
-        def second_positions(a, b):
-            codes, scales = c1_mx[a // half]
-            return codes[:, a % half : a % half + b - a].bitcast(FP8X4), scales[:, a % half : a % half + b - a]
-
-        def position_pass(g):
-            return (v_mx[g][0][:], v_mx[g][1][:]), (first_positions, second_positions)[g]
-
-        def content_pass(g):
-            return (u_mx[g][0][:], u_mx[g][1][:]), lambda a, b: (kw[g][:, 2 * a : 2 * b].bitcast(FP4X4), ks[g][:, a:b])
+        def keys(g, b):
+            h, a = divmod(b * BANK_N, HALF)
+            return kw[h][:, g, 2 * a : 2 * (a + BANK_N)].bitcast(FP4X4), ks[g][:, b * BANK_N : (b + 1) * BANK_N]
 
         acc = [psum.tile([P, BANK_N], F32, name=f"acc{b}") for b in range(BANKS)]
-        passes = [position_pass(0), position_pass(1), content_pass(0), content_pass(1)]
-        for i, (rows, moving) in enumerate(passes):
+        passes = [(v_mx[g], positions, g) for g in range(PASSES)] + [(u_mx[g], keys, g) for g in range(PASSES)]
+        for i, (rows, moving, g) in enumerate(passes):
             for b in range(BANKS):
-                codes, scales = moving(b * BANK_N, (b + 1) * BANK_N)
+                codes, scales = moving(g, b)
                 nc.tensor.matmul_mx(
                     out=acc[b][:],
-                    lhsT=rows[0].bitcast(FP8X4),
-                    lhsT_scale=rows[1],
+                    lhsT=rows[0][:].bitcast(FP8X4),
+                    lhsT_scale=rows[1][:],
                     rhs=codes,
                     rhs_scale=scales,
                     start=(i == 0),

@@ -15,9 +15,9 @@ ROWS_ON_VECTOR = 64
 PLANE_LOADS = ((0, 2), (2, 4), (4, 6), (6, 7), (7, 8))
 KIB = 1024
 STAGE_AT = {
-    "c0": 0, "ks_both": 0,
-    "ks_pool": 8, "picked1": 8, "v0_grouped": 10, "v1_grouped": 11, "kw_pairs0": 12, "kw_pairs1": 13, "u0_grouped": 13,
-    "u0_raw": 16, "u1_grouped": 16,
+    "ks_pool": 0, "kw_pool": 0,
+    "picked1": 8, "v0_grouped": 10, "v1_grouped": 11, "kw_pairs0": 12, "kw_pairs1": 13, "u0_grouped": 13,
+    "c2": 16, "v0_raw": 16, "v1_raw": 18, "u0_raw": 20, "u1_raw": 22, "u1_grouped": 20,
 }
 
 FLOPS = 2 * 2 * D * NQ * SLOTS
@@ -96,32 +96,37 @@ def tile_attend_txlseg_kernel(tc, uT, vT, k_words, k_scales, cT, offs, offs2, ou
         key_list = sb.tile([P, SLOTS // 16], U16, name="key_list")
         pos_list = sb.tile([P, SLOTS // 16], U16, name="pos_list")
         ks_pool = staged("ks_pool", [P, T // 4], I32)
-        ks_second = staged("ks_second", [P, SLOTS // 4], I32)
-        nc.vector.memset(ks_pool[:], 0)
-        nc.vector.memset(ks_second[:], 0)
+        ks_planes = staged("ks_planes", [P, PASSES, SLOTS // 4], I32)
+        nc.vector.memset(ks_pool[32:64, :], 0)
+        nc.vector.memset(ks_pool[64:P, :], 0)
+        nc.vector.memset(ks_planes[:], 0)
         load_planes(*PLANE_LOADS[0])
         nc.sync.dma_start(pos_list[:], offs2)
         nc.sync.dma_start(key_list[:], offs)
+        nc.sync.dma_start(out=ks_pool[0:32, :], in_=k_scales.rearrange("o f t -> (o f) t").bitcast(I32))
         for span in PLANE_LOADS[1:]:
             load_planes(*span)
-        kw_pool = staged("kw_pool", [P, T], I32)
-        nc.sync.dma_start(out=kw_pool[:], in_=k_words[0].rearrange("p t b -> p (t b)").bitcast(I32))
-        v_raw = [load_queries("v", vT, g) for g in range(PASSES)]
-        u_raw = [load_queries("u", uT, g) for g in range(PASSES)]
-        scale_rows = k_scales.rearrange("o (q r) t -> r q o t", r=4)
-        for r in range(4):
-            nc.gpsimd.dma_start(out=ks_pool[r:P:16, :], in_=scale_rows[r].bitcast(I32))
 
         picked0 = staged("picked0", [P, PACK, SLOTS], F32)
         for j in (0, 1):
             gather_plane(picked0, j, 0, SLOTS)
         ks_both = staged("ks_both", [P, SLOTS], U8)
         nc.vector.tensor_copy(out=ks_both[:], in_=ks_pool[:].bitcast(U8).indirect(key_list[:]))
-        for r in range(4):
-            nc.gpsimd.dma_start(out=ks_second[r:P:32, :], in_=ks_both[16 + r : P : 32, :].bitcast(I32))
-        ks = [ks_both[:], ks_second[:].bitcast(U8)]
+
+        def move_scales(g):
+            for q in range(4):
+                row = 16 * g + 4 * q
+                nc.sync.dma_start(out=ks_planes[32 * q : 32 * q + 4, g, :], in_=ks_both[row : row + 4, :].bitcast(I32))
+
+        move_scales(0)
+        kw_pool = staged("kw_pool", [P, T], I32)
+        nc.sync.dma_start(out=kw_pool[:], in_=k_words[0].rearrange("p t b -> p (t b)").bitcast(I32))
+        move_scales(1)
+        ks = [ks_planes[:, g, :].bitcast(U8) for g in range(PASSES)]
         gather_plane(picked0, 2, 0, SLOTS)
         grouped0 = group_positions(0, picked0)
+        v_raw = [load_queries("v", vT, g) for g in range(PASSES)]
+        u_raw = [load_queries("u", uT, g) for g in range(PASSES)]
         picked1 = staged("picked1", [P, PACK, SLOTS], F32)
         for j in (4, 5):
             gather_plane(picked1, j, 0, SLOTS)

@@ -16,8 +16,8 @@ PLANE_LOADS = ((0, 2), (2, 4), (4, 6), (6, 7), (7, 8))
 KIB = 1024
 STAGE_AT = {
     "ks_pool": 0, "kw_pool": 0,
-    "picked1": 8, "v0_grouped": 10, "v1_grouped": 11, "kw_pairs0": 12, "kw_pairs1": 13, "u0_grouped": 13,
-    "c2": 16, "v0_raw": 16, "v1_raw": 18, "u0_raw": 20, "u1_raw": 22, "u1_grouped": 20,
+    "picked1": 10, "v0_grouped": 12, "v1_grouped": 13, "kw_pairs0": 14, "kw_pairs1": 15, "u0_grouped": 15,
+    "v0_raw": 20.125, "c2": 22, "v1_raw": 22.5, "u0_raw": 25, "u1_raw": 27.5, "u1_grouped": 25,
 }
 
 FLOPS = 2 * 2 * D * NQ * SLOTS
@@ -49,7 +49,7 @@ def tile_attend_txlseg_kernel(tc, uT, vT, k_words, k_scales, cT, offs, offs2, ou
         def staged(name, shape, dtype):
             if name not in STAGE_AT:
                 return sb.tile(shape, dtype, name=name, align_bytes=64)
-            return stage.tile(shape, dtype, name=name, offset=STAGE_AT[name] * KIB, align_bytes=64)
+            return stage.tile(shape, dtype, name=name, offset=int(STAGE_AT[name] * KIB), align_bytes=64)
 
         c_rows = cT.rearrange("(g p t) n -> g p t n", p=P, t=PACK)
         windows = {}
@@ -95,33 +95,27 @@ def tile_attend_txlseg_kernel(tc, uT, vT, k_words, k_scales, cT, offs, offs2, ou
 
         key_list = sb.tile([P, SLOTS // 16], U16, name="key_list")
         pos_list = sb.tile([P, SLOTS // 16], U16, name="pos_list")
-        ks_pool = staged("ks_pool", [P, T // 4], I32)
+        ks_pool = staged("ks_pool", [P, PASSES, T // 4], I32)
         ks_planes = staged("ks_planes", [P, PASSES, SLOTS // 4], I32)
-        nc.vector.memset(ks_pool[32:64, :], 0)
-        nc.vector.memset(ks_pool[64:P, :], 0)
+        nc.vector.memset(ks_pool[:], 0)
         nc.vector.memset(ks_planes[:], 0)
         load_planes(*PLANE_LOADS[0])
         nc.sync.dma_start(pos_list[:], offs2)
         nc.sync.dma_start(key_list[:], offs)
-        nc.sync.dma_start(out=ks_pool[0:32, :], in_=k_scales.rearrange("o f t -> (o f) t").bitcast(I32))
+        nc.sync.dma_start(out=ks_pool[0:P:8], in_=k_scales.rearrange("o f t -> f o t").bitcast(I32))
         for span in PLANE_LOADS[1:]:
             load_planes(*span)
 
         picked0 = staged("picked0", [P, PACK, SLOTS], F32)
         for j in (0, 1):
             gather_plane(picked0, j, 0, SLOTS)
-        ks_both = staged("ks_both", [P, SLOTS], U8)
-        nc.vector.tensor_copy(out=ks_both[:], in_=ks_pool[:].bitcast(U8).indirect(key_list[:]))
-
-        def move_scales(g):
-            for q in range(4):
-                row = 16 * g + 4 * q
-                nc.sync.dma_start(out=ks_planes[32 * q : 32 * q + 4, g, :], in_=ks_both[row : row + 4, :].bitcast(I32))
-
-        move_scales(0)
+        ks_both = staged("ks_both", [P, PASSES, SLOTS], U8)
+        for g in range(PASSES):
+            nc.vector.tensor_copy(out=ks_both[:, g, :], in_=ks_pool[:, g, :].bitcast(U8).indirect(key_list[:]))
+        for q in range(0, P, 32):
+            nc.sync.dma_start(out=ks_planes[q : q + 4], in_=ks_both[q : q + 32 : 8].bitcast(I32))
         kw_pool = staged("kw_pool", [P, T], I32)
         nc.sync.dma_start(out=kw_pool[:], in_=k_words[0].rearrange("p t b -> p (t b)").bitcast(I32))
-        move_scales(1)
         ks = [ks_planes[:, g, :].bitcast(U8) for g in range(PASSES)]
         gather_plane(picked0, 2, 0, SLOTS)
         grouped0 = group_positions(0, picked0)
@@ -133,7 +127,7 @@ def tile_attend_txlseg_kernel(tc, uT, vT, k_words, k_scales, cT, offs, offs2, ou
         c_mx = [[quantize(f"c0{h}", grouped0[h][:], HALF) for h in range(2)]]
         gather_plane(picked1, 6, 0, SLOTS)
         grouped1 = group_positions(1, picked1)
-        c_mx.append([quantize(f"c1{h}", grouped1[h][:], HALF) for h in range(2)])
+        c_mx.append([quantize(f"c1{h}", grouped1[h][:], HALF) for h in (1, 0)][::-1])
 
         kw_pairs = [staged(f"kw_pairs{h}", [P, HALF], U32) for h in range(2)]
         for h in range(2):
@@ -147,7 +141,7 @@ def tile_attend_txlseg_kernel(tc, uT, vT, k_words, k_scales, cT, offs, offs2, ou
             )
         v_mx = [quantize("v0", group_queries("v0", v_raw[0], 0)[:], NQ)]
         v1_grouped = group_queries("v1", v_raw[1], 0)
-        u0_grouped = group_queries("u0", u_raw[0], ROWS_ON_VECTOR)
+        u0_grouped = group_queries("u0", u_raw[0][:], ROWS_ON_VECTOR)
         v_mx.append(quantize("v1", v1_grouped[:], NQ))
         u_mx = [quantize("u0", u0_grouped[:], NQ)]
         u_mx.append(quantize("u1", group_queries("u1", u_raw[1], ROWS_ON_VECTOR)[:], NQ))

@@ -77,14 +77,23 @@ def tile_attend_txlseg_kernel(tc, uT, vT, k_words, k_scales, cT, offs, offs2, ou
                 out=picked[:, j % PACK, s0:s1], in_=windows[j].indirect(pos_list[:, s0 // 16 : s1 // 16])
             )
 
-        def group_positions(g, picked):
-            gather_plane(picked, PACK * g + 3, 0, HALF)
-            first = staged(f"grouped{g}a", [P, HALF, PACK], BF16)
-            interleave(nc.scalar.copy, first[:], picked[:, :, :HALF])
-            gather_plane(picked, PACK * g + 3, HALF, SLOTS)
-            second = staged(f"grouped{g}b", [P, HALF, PACK], BF16)
-            interleave(nc.vector.tensor_copy, second[:], picked[:, :, HALF:])
-            return first, second
+        def group_pair(copy, grouped, picked, t):
+            for h in range(2):
+                interleave(copy, grouped[h][:, :, t : t + 2], picked[:, t : t + 2, h * HALF : (h + 1) * HALF])
+
+        def first_pair(g):
+            picked = staged(f"picked{g}", [P, PACK, SLOTS], F32)
+            for t in (0, 1):
+                gather_plane(picked, PACK * g + t, 0, SLOTS)
+            grouped = [staged(f"grouped{g}{h}", [P, HALF, PACK], BF16) for h in range(2)]
+            group_pair(nc.scalar.copy, grouped, picked, 0)
+            return picked, grouped
+
+        def second_pair(g, picked, grouped):
+            gather_plane(picked, PACK * g + 2, 0, SLOTS)
+            for s0 in (0, HALF):
+                gather_plane(picked, PACK * g + 3, s0, s0 + HALF)
+            group_pair(nc.vector.tensor_copy, grouped, picked, 2)
 
         def group_queries(name, raw, cut):
             grouped = staged(f"{name}_grouped", [P, NQ, PACK], BF16)
@@ -106,9 +115,7 @@ def tile_attend_txlseg_kernel(tc, uT, vT, k_words, k_scales, cT, offs, offs2, ou
         for span in PLANE_LOADS[1:]:
             load_planes(*span)
 
-        picked0 = staged("picked0", [P, PACK, SLOTS], F32)
-        for j in (0, 1):
-            gather_plane(picked0, j, 0, SLOTS)
+        picked0, grouped0 = first_pair(0)
         ks_both = staged("ks_both", [P, PASSES, SLOTS], U8)
         for g in range(PASSES):
             nc.vector.tensor_copy(out=ks_both[:, g, :], in_=ks_pool[:, g, :].bitcast(U8).indirect(key_list[:]))
@@ -117,17 +124,13 @@ def tile_attend_txlseg_kernel(tc, uT, vT, k_words, k_scales, cT, offs, offs2, ou
         kw_pool = staged("kw_pool", [P, T], I32)
         nc.sync.dma_start(out=kw_pool[:], in_=k_words[0].rearrange("p t b -> p (t b)").bitcast(I32))
         ks = [ks_planes[:, g, :].bitcast(U8) for g in range(PASSES)]
-        gather_plane(picked0, 2, 0, SLOTS)
-        grouped0 = group_positions(0, picked0)
+        second_pair(0, picked0, grouped0)
         v_raw = [load_queries("v", vT, g) for g in range(PASSES)]
         u_raw = [load_queries("u", uT, g) for g in range(PASSES)]
-        picked1 = staged("picked1", [P, PACK, SLOTS], F32)
-        for j in (4, 5):
-            gather_plane(picked1, j, 0, SLOTS)
+        picked1, grouped1 = first_pair(1)
         c_mx = [[quantize(f"c0{h}", grouped0[h][:], HALF) for h in range(2)]]
-        gather_plane(picked1, 6, 0, SLOTS)
-        grouped1 = group_positions(1, picked1)
-        c_mx.append([quantize(f"c1{h}", grouped1[h][:], HALF) for h in (1, 0)][::-1])
+        second_pair(1, picked1, grouped1)
+        c_mx.append([quantize(f"c1{h}", grouped1[h][:], HALF) for h in range(2)])
 
         kw_pairs = [staged(f"kw_pairs{h}", [P, HALF], U32) for h in range(2)]
         for h in range(2):

@@ -10,7 +10,7 @@ PASSES = D // K_PASS
 BANK_N = 128
 BANKS = SLOTS // BANK_N
 HALF = SLOTS // 2
-RUN = 4
+RUN = 2
 ROWS_ON_VECTOR = 64
 PLANE_LOADS = ((0, 2), (2, 4), (4, 6), (6, 7), (7, 8))
 KIB = 1024

@@ -13,6 +13,7 @@ HALF = SLOTS // 2
 RUN = 2
 ROWS_ON_VECTOR = 64
 PLANE_LOADS = ((0, 2), (2, 4), (4, 6), (6, 7), (7, 8))
+ROW0, ROW_STEP = 11, 7
 KIB = 1024
 STAGE_AT = {
     "ks_pool": 0, "kw_pool": 0,
@@ -111,7 +112,7 @@ def tile_attend_txlseg_kernel(tc, uT, vT, k_words, k_scales, cT, offs, offs2, ou
         load_planes(*PLANE_LOADS[0])
         nc.sync.dma_start(pos_list[:], offs2)
         nc.sync.dma_start(key_list[:], offs)
-        nc.sync.dma_start(out=ks_pool[0:P:8], in_=k_scales.rearrange("o f t -> f o t").bitcast(I32))
+        nc.sync.dma_start(out=ks_pool[ROW0 : ROW0 + 16 * ROW_STEP : ROW_STEP], in_=k_scales.rearrange("o f t -> f o t").bitcast(I32))
         for span in PLANE_LOADS[1:]:
             load_planes(*span)
 
@@ -119,8 +120,9 @@ def tile_attend_txlseg_kernel(tc, uT, vT, k_words, k_scales, cT, offs, offs2, ou
         ks_both = staged("ks_both", [P, PASSES, SLOTS], U8)
         for g in range(PASSES):
             nc.vector.tensor_copy(out=ks_both[:, g, :], in_=ks_pool[:, g, :].bitcast(U8).indirect(key_list[:]))
-        for q in range(0, P, 32):
-            nc.sync.dma_start(out=ks_planes[q : q + 4], in_=ks_both[q : q + 32 : 8].bitcast(I32))
+        for r in range(4):
+            first = ROW0 + r * ROW_STEP
+            nc.sync.dma_start(out=ks_planes[r:P:32], in_=ks_both[first : first + 13 * ROW_STEP : 4 * ROW_STEP].bitcast(I32))
         kw_pool = staged("kw_pool", [P, T], I32)
         nc.sync.dma_start(out=kw_pool[:], in_=k_words[0].rearrange("p t b -> p (t b)").bitcast(I32))
         ks = [ks_planes[:, g, :].bitcast(U8) for g in range(PASSES)]

@@ -73,10 +73,12 @@ def tile_attend_txlseg_kernel(tc, uT, vT, k_words, k_scales, cT, offs, offs2, ou
             nc.vector.quantize_mx(out=codes[:].bitcast(FP8X4), scales=scales[:], in_=grouped.rearrange("p n t -> p (n t)"))
             return codes, scales
 
-        def gather_plane(picked, j, s0, s1):
-            nc.vector.tensor_copy(
-                out=picked[:, j % PACK, s0:s1], in_=windows[j].indirect(pos_list[:, s0 // 16 : s1 // 16])
-            )
+        def gather_plane(picked, j, s0, s1, on_scalar=False):
+            dst, src = picked[:, j % PACK, s0:s1], windows[j].indirect(pos_list[:, s0 // 16 : s1 // 16])
+            if on_scalar:
+                nc.scalar.activation(out=dst, in_=src, func=mybir.ActivationFunctionType.Copy)
+            else:
+                nc.vector.tensor_copy(out=dst, in_=src)
 
         def group_pair(copy, grouped, picked, t):
             for h in range(2):
@@ -84,8 +86,11 @@ def tile_attend_txlseg_kernel(tc, uT, vT, k_words, k_scales, cT, offs, offs2, ou
 
         def first_pair(g):
             picked = staged(f"picked{g}", [P, PACK, SLOTS], F32)
-            for t in (0, 1):
-                gather_plane(picked, PACK * g + t, 0, SLOTS)
+            gather_plane(picked, PACK * g, 0, SLOTS)
+            cut = HALF if g else SLOTS
+            gather_plane(picked, PACK * g + 1, 0, cut)
+            if g:
+                gather_plane(picked, PACK * g + 1, cut, SLOTS, on_scalar=True)
             grouped = [staged(f"grouped{g}{h}", [P, HALF, PACK], BF16) for h in range(2)]
             group_pair(nc.scalar.copy, grouped, picked, 0)
             return picked, grouped

@@ -12,13 +12,13 @@ BANKS = SLOTS // BANK_N
 HALF = SLOTS // 2
 RUN = 2
 ROWS_ON_VECTOR = 64
-PLANE_LOADS = ((0, 2), (2, 4), (4, 6), (6, 7), (7, 8))
-ROW0, ROW_STEP = 11, 7
+SLOTS_ON_SCALAR = 128
+PLANE_LOADS = ((0, 4), (4, 7), (7, 8))
+ROW_STEP = 8
 KIB = 1024
 STAGE_AT = {
-    "ks_pool": 0, "kw_pool": 0,
-    "picked1": 10, "v0_grouped": 12, "v1_grouped": 13, "kw_pairs0": 14, "kw_pairs1": 15, "u0_grouped": 15,
-    "v0_raw": 20.125, "c2": 22, "v1_raw": 22.5, "u0_raw": 25, "u1_raw": 27.5, "u1_grouped": 25,
+    "ks_pool": 0, "grouped01": 0, "u1_raw": 0, "grouped00": 2, "picked1": 2,
+    "v0_grouped": 3, "v1_grouped": 4, "u0_grouped": 5, "u1_grouped": 6, "kw_pairs0": 7, "kw_pairs1": 8,
 }
 
 FLOPS = 2 * 2 * D * NQ * SLOTS
@@ -73,33 +73,12 @@ def tile_attend_txlseg_kernel(tc, uT, vT, k_words, k_scales, cT, offs, offs2, ou
             nc.vector.quantize_mx(out=codes[:].bitcast(FP8X4), scales=scales[:], in_=grouped.rearrange("p n t -> p (n t)"))
             return codes, scales
 
-        def gather_plane(picked, j, s0, s1, on_scalar=False):
+        def gather_plane(picked, j, s0, s1, on_scalar):
             dst, src = picked[:, j % PACK, s0:s1], windows[j].indirect(pos_list[:, s0 // 16 : s1 // 16])
             if on_scalar:
                 nc.scalar.activation(out=dst, in_=src, func=mybir.ActivationFunctionType.Copy)
             else:
                 nc.vector.tensor_copy(out=dst, in_=src)
-
-        def group_pair(copy, grouped, picked, t):
-            for h in range(2):
-                interleave(copy, grouped[h][:, :, t : t + 2], picked[:, t : t + 2, h * HALF : (h + 1) * HALF])
-
-        def first_pair(g):
-            picked = staged(f"picked{g}", [P, PACK, SLOTS], F32)
-            gather_plane(picked, PACK * g, 0, SLOTS)
-            cut = HALF if g else SLOTS
-            gather_plane(picked, PACK * g + 1, 0, cut)
-            if g:
-                gather_plane(picked, PACK * g + 1, cut, SLOTS, on_scalar=True)
-            grouped = [staged(f"grouped{g}{h}", [P, HALF, PACK], BF16) for h in range(2)]
-            group_pair(nc.scalar.copy, grouped, picked, 0)
-            return picked, grouped
-
-        def second_pair(g, picked, grouped):
-            gather_plane(picked, PACK * g + 2, 0, SLOTS)
-            for s0 in (0, HALF):
-                gather_plane(picked, PACK * g + 3, s0, s0 + HALF)
-            group_pair(nc.vector.tensor_copy, grouped, picked, 2)
 
         def group_queries(name, raw, cut):
             grouped = staged(f"{name}_grouped", [P, NQ, PACK], BF16)
@@ -111,32 +90,50 @@ def tile_attend_txlseg_kernel(tc, uT, vT, k_words, k_scales, cT, offs, offs2, ou
         key_list = sb.tile([P, SLOTS // 16], U16, name="key_list")
         pos_list = sb.tile([P, SLOTS // 16], U16, name="pos_list")
         ks_pool = staged("ks_pool", [P, PASSES, T // 4], I32)
-        ks_planes = staged("ks_planes", [P, PASSES, SLOTS // 4], I32)
         nc.vector.memset(ks_pool[:], 0)
-        nc.vector.memset(ks_planes[:], 0)
-        load_planes(*PLANE_LOADS[0])
+        warm = sb.tile([P, 2], F32, name="warm")
+        nc.gpsimd.memset(warm[:, 0:1], 0.0)
+        nc.scalar.activation(out=warm[:, 1:2], in_=warm[:, 0:1], func=mybir.ActivationFunctionType.Copy)
         nc.sync.dma_start(pos_list[:], offs2)
+        load_planes(*PLANE_LOADS[0])
         nc.sync.dma_start(key_list[:], offs)
-        nc.sync.dma_start(out=ks_pool[ROW0 : ROW0 + 16 * ROW_STEP : ROW_STEP], in_=k_scales.rearrange("o f t -> f o t").bitcast(I32))
+        nc.sync.dma_start(out=ks_pool[0:P:ROW_STEP], in_=k_scales.rearrange("o f t -> f o t").bitcast(I32))
         for span in PLANE_LOADS[1:]:
             load_planes(*span)
+        kw_pool = staged("kw_pool", [P, T], I32)
+        nc.sync.dma_start(out=kw_pool[:], in_=k_words[0].rearrange("p t b -> p (t b)").bitcast(I32))
+        v_raw = [load_queries("v", vT, g) for g in range(PASSES)]
+        u_raw = [load_queries("u", uT, 0)]
 
-        picked0, grouped0 = first_pair(0)
+        picked0 = staged("picked0", [P, PACK, SLOTS], F32)
+        for j in range(PACK):
+            gather_plane(picked0, j, 0, SLOTS, on_scalar=j > 0)
         ks_both = staged("ks_both", [P, PASSES, SLOTS], U8)
         for g in range(PASSES):
             nc.vector.tensor_copy(out=ks_both[:, g, :], in_=ks_pool[:, g, :].bitcast(U8).indirect(key_list[:]))
-        for r in range(4):
-            first = ROW0 + r * ROW_STEP
-            nc.sync.dma_start(out=ks_planes[r:P:32], in_=ks_both[first : first + 13 * ROW_STEP : 4 * ROW_STEP].bitcast(I32))
-        kw_pool = staged("kw_pool", [P, T], I32)
-        nc.sync.dma_start(out=kw_pool[:], in_=k_words[0].rearrange("p t b -> p (t b)").bitcast(I32))
+        ks_planes = staged("ks_planes", [P, PASSES, SLOTS // 4], I32)
+        nc.vector.tensor_copy(out=ks_planes[:], in_=ks_both[:].bitcast(I32))
+        for r in range(1, 4):
+            nc.sync.dma_start(out=ks_planes[r:P:32], in_=ks_both[r * ROW_STEP : P : 32].bitcast(I32))
         ks = [ks_planes[:, g, :].bitcast(U8) for g in range(PASSES)]
-        second_pair(0, picked0, grouped0)
-        v_raw = [load_queries("v", vT, g) for g in range(PASSES)]
-        u_raw = [load_queries("u", uT, g) for g in range(PASSES)]
-        picked1, grouped1 = first_pair(1)
+
+        grouped0 = [staged(f"grouped0{h}", [P, HALF, PACK], BF16) for h in range(2)]
+        for h in range(2):
+            interleave(nc.vector.tensor_copy, grouped0[h][:], picked0[:, :, h * HALF : (h + 1) * HALF])
         c_mx = [[quantize(f"c0{h}", grouped0[h][:], HALF) for h in range(2)]]
-        second_pair(1, picked1, grouped1)
+        u_raw.append(load_queries("u", uT, 1))
+
+        picked1 = staged("picked1", [P, PACK, SLOTS], F32)
+        gather_plane(picked1, 4, 0, SLOTS, on_scalar=False)
+        for j in (5, 6):
+            gather_plane(picked1, j, 0, SLOTS, on_scalar=True)
+        gather_plane(picked1, 7, 0, HALF, on_scalar=False)
+        gather_plane(picked1, 7, HALF, SLOTS, on_scalar=True)
+        grouped1 = [staged(f"grouped1{h}", [P, HALF, PACK], BF16) for h in range(2)]
+        cut = HALF - SLOTS_ON_SCALAR
+        interleave(nc.vector.tensor_copy, grouped1[0][:], picked1[:, :, :HALF])
+        interleave(nc.scalar.copy, grouped1[1][:, cut:, :], picked1[:, :, HALF + cut :])
+        interleave(nc.vector.tensor_copy, grouped1[1][:, :cut, :], picked1[:, :, HALF : HALF + cut])
         c_mx.append([quantize(f"c1{h}", grouped1[h][:], HALF) for h in range(2)])
 
         kw_pairs = [staged(f"kw_pairs{h}", [P, HALF], U32) for h in range(2)]

@@ -13,12 +13,12 @@ HALF = SLOTS // 2
 RUN = 2
 ROWS_ON_VECTOR = 64
 SLOTS_ON_SCALAR = 128
-PLANE_LOADS = ((0, 4), (4, 7), (7, 8))
+PLANE_LOADS = ((0, 1), (1, 4), (4, 7), (7, 8))
 ROW_STEP = 8
 KIB = 1024
 STAGE_AT = {
-    "ks_pool": 0, "grouped01": 0, "u1_raw": 0, "grouped00": 2, "picked1": 2,
-    "v0_grouped": 3, "v1_grouped": 4, "u0_grouped": 5, "u1_grouped": 6, "kw_pairs0": 7, "kw_pairs1": 8,
+    "grouped00": 0, "picked1": 0,
+    "v0_grouped": 1, "v1_grouped": 2, "u0_grouped": 3, "u1_grouped": 4, "kw_pairs0": 5, "kw_pairs1": 6,
 }
 
 FLOPS = 2 * 2 * D * NQ * SLOTS
@@ -91,13 +91,10 @@ def tile_attend_txlseg_kernel(tc, uT, vT, k_words, k_scales, cT, offs, offs2, ou
         pos_list = sb.tile([P, SLOTS // 16], U16, name="pos_list")
         ks_pool = staged("ks_pool", [P, PASSES, T // 4], I32)
         nc.vector.memset(ks_pool[:], 0)
-        warm = sb.tile([P, 2], F32, name="warm")
-        nc.gpsimd.memset(warm[:, 0:1], 0.0)
-        nc.scalar.activation(out=warm[:, 1:2], in_=warm[:, 0:1], func=mybir.ActivationFunctionType.Copy)
-        nc.sync.dma_start(pos_list[:], offs2)
         load_planes(*PLANE_LOADS[0])
         nc.sync.dma_start(key_list[:], offs)
         nc.sync.dma_start(out=ks_pool[0:P:ROW_STEP], in_=k_scales.rearrange("o f t -> f o t").bitcast(I32))
+        nc.sync.dma_start(pos_list[:], offs2)
         for span in PLANE_LOADS[1:]:
             load_planes(*span)
         kw_pool = staged("kw_pool", [P, T], I32)
@@ -105,9 +102,6 @@ def tile_attend_txlseg_kernel(tc, uT, vT, k_words, k_scales, cT, offs, offs2, ou
         v_raw = [load_queries("v", vT, g) for g in range(PASSES)]
         u_raw = [load_queries("u", uT, 0)]
 
-        picked0 = staged("picked0", [P, PACK, SLOTS], F32)
-        for j in range(PACK):
-            gather_plane(picked0, j, 0, SLOTS, on_scalar=j > 0)
         ks_both = staged("ks_both", [P, PASSES, SLOTS], U8)
         for g in range(PASSES):
             nc.vector.tensor_copy(out=ks_both[:, g, :], in_=ks_pool[:, g, :].bitcast(U8).indirect(key_list[:]))
@@ -116,25 +110,24 @@ def tile_attend_txlseg_kernel(tc, uT, vT, k_words, k_scales, cT, offs, offs2, ou
         for r in range(1, 4):
             nc.sync.dma_start(out=ks_planes[r:P:32], in_=ks_both[r * ROW_STEP : P : 32].bitcast(I32))
         ks = [ks_planes[:, g, :].bitcast(U8) for g in range(PASSES)]
-
-        grouped0 = [staged(f"grouped0{h}", [P, HALF, PACK], BF16) for h in range(2)]
-        for h in range(2):
-            interleave(nc.vector.tensor_copy, grouped0[h][:], picked0[:, :, h * HALF : (h + 1) * HALF])
-        c_mx = [[quantize(f"c0{h}", grouped0[h][:], HALF) for h in range(2)]]
         u_raw.append(load_queries("u", uT, 1))
 
-        picked1 = staged("picked1", [P, PACK, SLOTS], F32)
-        gather_plane(picked1, 4, 0, SLOTS, on_scalar=False)
-        for j in (5, 6):
-            gather_plane(picked1, j, 0, SLOTS, on_scalar=True)
-        gather_plane(picked1, 7, 0, HALF, on_scalar=False)
-        gather_plane(picked1, 7, HALF, SLOTS, on_scalar=True)
-        grouped1 = [staged(f"grouped1{h}", [P, HALF, PACK], BF16) for h in range(2)]
-        cut = HALF - SLOTS_ON_SCALAR
-        interleave(nc.vector.tensor_copy, grouped1[0][:], picked1[:, :, :HALF])
-        interleave(nc.scalar.copy, grouped1[1][:, cut:, :], picked1[:, :, HALF + cut :])
-        interleave(nc.vector.tensor_copy, grouped1[1][:, :cut, :], picked1[:, :, HALF : HALF + cut])
-        c_mx.append([quantize(f"c1{h}", grouped1[h][:], HALF) for h in range(2)])
+        def position_pass(g, on_scalar, on_vector, shared):
+            picked = staged(f"picked{g}", [P, PACK, SLOTS], F32)
+            gather_plane(picked, on_vector, 0, SLOTS, on_scalar=False)
+            for j in on_scalar:
+                gather_plane(picked, j, 0, SLOTS, on_scalar=True)
+            for j in shared:
+                gather_plane(picked, j, 0, HALF, on_scalar=False)
+                gather_plane(picked, j, HALF, SLOTS, on_scalar=True)
+            grouped = [staged(f"grouped{g}{h}", [P, HALF, PACK], BF16) for h in range(2)]
+            cut = HALF - SLOTS_ON_SCALAR
+            interleave(nc.vector.tensor_copy, grouped[0][:], picked[:, :, :HALF])
+            interleave(nc.scalar.copy, grouped[1][:, cut:, :], picked[:, :, HALF + cut :])
+            interleave(nc.vector.tensor_copy, grouped[1][:, :cut, :], picked[:, :, HALF : HALF + cut])
+            return [quantize(f"c{g}{h}", grouped[h][:], HALF) for h in range(2)]
+
+        c_mx = [position_pass(0, (0, 2), 1, (3,)), position_pass(1, (5,), 4, (6, 7))]
 
         kw_pairs = [staged(f"kw_pairs{h}", [P, HALF], U32) for h in range(2)]
         for h in range(2):

@@ -7,12 +7,13 @@ PACK = 4
 K_PASS = P * PACK
 D, T, C, NQ, SLOTS, SEG = 1024, 2048, 1024, 128, 512, 32
 PASSES = D // K_PASS
-BANK_N = 128
+BANK_N = 256
 BANKS = SLOTS // BANK_N
 HALF = SLOTS // 2
 RUN = 2
-ROWS_ON_VECTOR = 64
-SLOTS_ON_SCALAR = 128
+ROWS_ON_VECTOR = 96
+SLOTS_ON_SCALAR = 192
+QUARTER = SLOTS // 4
 PLANE_LOADS = ((0, 1), (1, 4), (4, 7), (7, 8))
 ROW_STEP = 8
 KIB = 1024
@@ -120,6 +121,10 @@ def tile_attend_txlseg_kernel(tc, uT, vT, k_words, k_scales, cT, offs, offs2, ou
             for j in shared:
                 gather_plane(picked, j, 0, HALF, on_scalar=False)
                 gather_plane(picked, j, HALF, SLOTS, on_scalar=True)
+            last = PACK * g + PACK - 1
+            gather_plane(picked, last, 0, QUARTER, on_scalar=False)
+            gather_plane(picked, last, QUARTER, HALF, on_scalar=True)
+            gather_plane(picked, last, HALF, SLOTS, on_scalar=True)
             grouped = [staged(f"grouped{g}{h}", [P, HALF, PACK], BF16) for h in range(2)]
             cut = HALF - SLOTS_ON_SCALAR
             interleave(nc.vector.tensor_copy, grouped[0][:], picked[:, :, :HALF])
@@ -127,7 +132,7 @@ def tile_attend_txlseg_kernel(tc, uT, vT, k_words, k_scales, cT, offs, offs2, ou
             interleave(nc.vector.tensor_copy, grouped[1][:, :cut, :], picked[:, :, HALF : HALF + cut])
             return [quantize(f"c{g}{h}", grouped[h][:], HALF) for h in range(2)]
 
-        c_mx = [position_pass(0, (0, 2), 1, (3,)), position_pass(1, (5,), 4, (6, 7))]
+        c_mx = [position_pass(0, (0, 2), 1, ()), position_pass(1, (5,), 4, (6,))]
 
         kw_pairs = [staged(f"kw_pairs{h}", [P, HALF], U32) for h in range(2)]
         for h in range(2):

@@ -7,7 +7,7 @@ PACK = 4
 K_PASS = P * PACK
 D, T, C, NQ, SLOTS, SEG = 1024, 2048, 1024, 128, 512, 32
 PASSES = D // K_PASS
-BANK_N = 256
+BANK_N = 128
 BANKS = SLOTS // BANK_N
 HALF = SLOTS // 2
 RUN = 2

@@ -11,15 +11,15 @@ BANK_N = 128
 BANKS = SLOTS // BANK_N
 HALF = SLOTS // 2
 RUN = 2
-ROWS_ON_VECTOR = 96
+ROWS_ON_VECTOR = {"v0": 0, "v1": 32, "u0": 48, "u1": 64}
 SLOTS_ON_SCALAR = 192
 QUARTER = SLOTS // 4
-PLANE_LOADS = ((0, 1), (1, 4), (4, 7), (7, 8))
+PLANE_LOADS = ((0, 4), (4, 7), (7, 8))
 ROW_STEP = 8
 KIB = 1024
 STAGE_AT = {
     "grouped00": 0, "picked1": 0,
-    "v0_grouped": 1, "v1_grouped": 2, "u0_grouped": 3, "u1_grouped": 4, "kw_pairs0": 5, "kw_pairs1": 6,
+    "v1_grouped": 2, "u0_grouped": 3, "u1_grouped": 4, "kw_pairs0": 5, "kw_pairs1": 6,
 }
 
 FLOPS = 2 * 2 * D * NQ * SLOTS
@@ -81,7 +81,8 @@ def tile_attend_txlseg_kernel(tc, uT, vT, k_words, k_scales, cT, offs, offs2, ou
             else:
                 nc.vector.tensor_copy(out=dst, in_=src)
 
-        def group_queries(name, raw, cut):
+        def group_queries(name, raw):
+            cut = ROWS_ON_VECTOR[name]
             grouped = staged(f"{name}_grouped", [P, NQ, PACK], BF16)
             interleave(nc.scalar.copy, grouped[:, cut:, :], raw[:, :, cut:])
             if cut:
@@ -92,17 +93,18 @@ def tile_attend_txlseg_kernel(tc, uT, vT, k_words, k_scales, cT, offs, offs2, ou
         pos_list = sb.tile([P, SLOTS // 16], U16, name="pos_list")
         ks_pool = staged("ks_pool", [P, PASSES, T // 4], I32)
         nc.vector.memset(ks_pool[:], 0)
-        load_planes(*PLANE_LOADS[0])
+        v_raw = [load_queries("v", vT, 0)]
         nc.sync.dma_start(key_list[:], offs)
-        nc.sync.dma_start(out=ks_pool[0:P:ROW_STEP], in_=k_scales.rearrange("o f t -> f o t").bitcast(I32))
         nc.sync.dma_start(pos_list[:], offs2)
-        for span in PLANE_LOADS[1:]:
+        nc.sync.dma_start(out=ks_pool[0:P:ROW_STEP], in_=k_scales.rearrange("o f t -> f o t").bitcast(I32))
+        for span in PLANE_LOADS:
             load_planes(*span)
         kw_pool = staged("kw_pool", [P, T], I32)
         nc.sync.dma_start(out=kw_pool[:], in_=k_words[0].rearrange("p t b -> p (t b)").bitcast(I32))
-        v_raw = [load_queries("v", vT, g) for g in range(PASSES)]
+        v_raw.append(load_queries("v", vT, 1))
         u_raw = [load_queries("u", uT, 0)]
 
+        v_mx = [quantize("v0", group_queries("v0", v_raw[0])[:], NQ)]
         ks_both = staged("ks_both", [P, PASSES, SLOTS], U8)
         for g in range(PASSES):
             nc.vector.tensor_copy(out=ks_both[:, g, :], in_=ks_pool[:, g, :].bitcast(U8).indirect(key_list[:]))
@@ -132,7 +134,7 @@ def tile_attend_txlseg_kernel(tc, uT, vT, k_words, k_scales, cT, offs, offs2, ou
             interleave(nc.vector.tensor_copy, grouped[1][:, :cut, :], picked[:, :, HALF : HALF + cut])
             return [quantize(f"c{g}{h}", grouped[h][:], HALF) for h in range(2)]
 
-        c_mx = [position_pass(0, (0, 2), 1, ()), position_pass(1, (5,), 4, (6,))]
+        c_mx = [position_pass(0, (1,), 0, (2,)), position_pass(1, (5,), 4, (6,))]
 
         kw_pairs = [staged(f"kw_pairs{h}", [P, HALF], U32) for h in range(2)]
         for h in range(2):
@@ -140,16 +142,17 @@ def tile_attend_txlseg_kernel(tc, uT, vT, k_words, k_scales, cT, offs, offs2, ou
                 out=kw_pairs[h][:], in_=kw_pool[:].bitcast(U32).indirect(key_list[:, h * HALF // 16 : (h + 1) * HALF // 16])
             )
         kw = [staged(f"kw{h}", [P, PASSES, 2 * HALF], U8) for h in range(2)]
-        for h in range(2):
+
+        def part_words(h):
             nc.vector.tensor_copy(
                 out=kw[h][:].bitcast(U16), in_=kw_pairs[h][:].bitcast(U16).rearrange("p (n o) -> p o n", o=PASSES)
             )
-        v_mx = [quantize("v0", group_queries("v0", v_raw[0], 0)[:], NQ)]
-        v1_grouped = group_queries("v1", v_raw[1], 0)
-        u0_grouped = group_queries("u0", u_raw[0][:], ROWS_ON_VECTOR)
+
+        part_words(0)
+        v1_grouped = group_queries("v1", v_raw[1])
+        part_words(1)
         v_mx.append(quantize("v1", v1_grouped[:], NQ))
-        u_mx = [quantize("u0", u0_grouped[:], NQ)]
-        u_mx.append(quantize("u1", group_queries("u1", u_raw[1], ROWS_ON_VECTOR)[:], NQ))
+        u_mx = [quantize(f"u{g}", group_queries(f"u{g}", u_raw[g])[:], NQ) for g in range(PASSES)]
 
         def positions(g, b):
             h, a = divmod(b * BANK_N, HALF)

@@ -11,7 +11,7 @@ BANK_N = 128
 BANKS = SLOTS // BANK_N
 HALF = SLOTS // 2
 RUN = 2
-ROWS_ON_VECTOR = {"v0": 0, "v1": 32, "u0": 48, "u1": 64}
+ROWS_ON_VECTOR = {"v0": 0, "v1": 0, "u0": 48, "u1": 64}
 SLOTS_ON_SCALAR = 192
 QUARTER = SLOTS // 4
 PLANE_LOADS = ((0, 4), (4, 7), (7, 8))
@@ -19,7 +19,7 @@ ROW_STEP = 8
 KIB = 1024
 STAGE_AT = {
     "grouped00": 0, "picked1": 0,
-    "v1_grouped": 2, "u0_grouped": 3, "u1_grouped": 4, "kw_pairs0": 5, "kw_pairs1": 6,
+    "u0_grouped": 3, "u1_grouped": 4, "kw_pairs0": 5, "kw_pairs1": 6,
 }
 
 FLOPS = 2 * 2 * D * NQ * SLOTS
@@ -93,7 +93,8 @@ def tile_attend_txlseg_kernel(tc, uT, vT, k_words, k_scales, cT, offs, offs2, ou
         pos_list = sb.tile([P, SLOTS // 16], U16, name="pos_list")
         ks_pool = staged("ks_pool", [P, PASSES, T // 4], I32)
         nc.vector.memset(ks_pool[:], 0)
-        v_raw = [load_queries("v", vT, 0)]
+        v_raw = staged("v_raw", [P, PASSES, PACK, NQ], F32)
+        nc.sync.dma_start(out=v_raw[:], in_=vT[0].rearrange("(g p t) q -> p g t q", p=P, t=PACK))
         nc.sync.dma_start(key_list[:], offs)
         nc.sync.dma_start(pos_list[:], offs2)
         nc.sync.dma_start(out=ks_pool[0:P:ROW_STEP], in_=k_scales.rearrange("o f t -> f o t").bitcast(I32))
@@ -101,10 +102,9 @@ def tile_attend_txlseg_kernel(tc, uT, vT, k_words, k_scales, cT, offs, offs2, ou
             load_planes(*span)
         kw_pool = staged("kw_pool", [P, T], I32)
         nc.sync.dma_start(out=kw_pool[:], in_=k_words[0].rearrange("p t b -> p (t b)").bitcast(I32))
-        v_raw.append(load_queries("v", vT, 1))
         u_raw = [load_queries("u", uT, 0)]
 
-        v_mx = [quantize("v0", group_queries("v0", v_raw[0])[:], NQ)]
+        v_mx = [quantize(f"v{g}", group_queries(f"v{g}", v_raw[:, g])[:], NQ) for g in range(PASSES)]
         ks_both = staged("ks_both", [P, PASSES, SLOTS], U8)
         for g in range(PASSES):
             nc.vector.tensor_copy(out=ks_both[:, g, :], in_=ks_pool[:, g, :].bitcast(U8).indirect(key_list[:]))
@@ -149,10 +149,9 @@ def tile_attend_txlseg_kernel(tc, uT, vT, k_words, k_scales, cT, offs, offs2, ou
             )
 
         part_words(0)
-        v1_grouped = group_queries("v1", v_raw[1])
+        u0_grouped = group_queries("u0", u_raw[0])
         part_words(1)
-        v_mx.append(quantize("v1", v1_grouped[:], NQ))
-        u_mx = [quantize(f"u{g}", group_queries(f"u{g}", u_raw[g])[:], NQ) for g in range(PASSES)]
+        u_mx = [quantize("u0", u0_grouped[:], NQ), quantize("u1", group_queries("u1", u_raw[1])[:], NQ)]
 
         def positions(g, b):
             h, a = divmod(b * BANK_N, HALF)
@@ -164,7 +163,7 @@ def tile_attend_txlseg_kernel(tc, uT, vT, k_words, k_scales, cT, offs, offs2, ou
             return kw[h][:, g, 2 * a : 2 * (a + BANK_N)].bitcast(FP4X4), ks[g][:, b * BANK_N : (b + 1) * BANK_N]
 
         acc = [psum.tile([P, BANK_N], F32, name=f"acc{b}") for b in range(BANKS)]
-        passes = [(v_mx[g], positions, g) for g in range(PASSES)] + [(u_mx[g], keys, g) for g in range(PASSES)]
+        passes = [(v_mx[g], positions, g) for g in reversed(range(PASSES))] + [(u_mx[g], keys, g) for g in range(PASSES)]
         for i, (rows, moving, g) in enumerate(passes):
             for b in range(BANKS):
                 codes, scales = moving(g, b)

@@ -145,7 +145,8 @@ def tile_attend_txlseg_kernel(tc, uT, vT, k_words, k_scales, cT, offs, offs2, ou
 
         def part_words(h):
             nc.vector.tensor_copy(
-                out=kw[h][:].bitcast(U16), in_=kw_pairs[h][:].bitcast(U16).rearrange("p (n o) -> p o n", o=PASSES)
+                out=kw[h][:].bitcast(U16).rearrange("p o (a n) -> p a o n", a=2),
+                in_=kw_pairs[h][:].bitcast(U16).rearrange("p (a n o) -> p a o n", a=2, o=PASSES),
             )
 
         part_words(0)

@@ -11,7 +11,7 @@ BANK_N = 128
 BANKS = SLOTS // BANK_N
 HALF = SLOTS // 2
 RUN = 2
-ROWS_ON_VECTOR = {"v0": 0, "v1": 0, "u0": 48, "u1": 64}
+ROWS_ON_VECTOR = {"v0": 0, "v1": 0, "u0": 0, "u1": 56}
 SLOTS_ON_SCALAR = 192
 QUARTER = SLOTS // 4
 PLANE_LOADS = ((0, 4), (4, 7), (7, 8))
@@ -100,9 +100,6 @@ def tile_attend_txlseg_kernel(tc, uT, vT, k_words, k_scales, cT, offs, offs2, ou
         nc.sync.dma_start(out=ks_pool[0:P:ROW_STEP], in_=k_scales.rearrange("o f t -> f o t").bitcast(I32))
         for span in PLANE_LOADS:
             load_planes(*span)
-        kw_pool = staged("kw_pool", [P, T], I32)
-        nc.sync.dma_start(out=kw_pool[:], in_=k_words[0].rearrange("p t b -> p (t b)").bitcast(I32))
-        u_raw = [load_queries("u", uT, 0)]
 
         v_mx = [quantize(f"v{g}", group_queries(f"v{g}", v_raw[:, g])[:], NQ) for g in range(PASSES)]
         ks_both = staged("ks_both", [P, PASSES, SLOTS], U8)
@@ -113,7 +110,9 @@ def tile_attend_txlseg_kernel(tc, uT, vT, k_words, k_scales, cT, offs, offs2, ou
         for r in range(1, 4):
             nc.sync.dma_start(out=ks_planes[r:P:32], in_=ks_both[r * ROW_STEP : P : 32].bitcast(I32))
         ks = [ks_planes[:, g, :].bitcast(U8) for g in range(PASSES)]
-        u_raw.append(load_queries("u", uT, 1))
+        kw_pool = staged("kw_pool", [P, T], I32)
+        nc.sync.dma_start(out=kw_pool[:], in_=k_words[0].rearrange("p t b -> p (t b)").bitcast(I32))
+        u_raw = [load_queries("u", uT, g) for g in range(PASSES)]
 
         def position_pass(g, on_scalar, on_vector, shared):
             picked = staged(f"picked{g}", [P, PACK, SLOTS], F32)
@@ -142,17 +141,13 @@ def tile_attend_txlseg_kernel(tc, uT, vT, k_words, k_scales, cT, offs, offs2, ou
                 out=kw_pairs[h][:], in_=kw_pool[:].bitcast(U32).indirect(key_list[:, h * HALF // 16 : (h + 1) * HALF // 16])
             )
         kw = [staged(f"kw{h}", [P, PASSES, 2 * HALF], U8) for h in range(2)]
-
-        def part_words(h):
+        for h in range(2):
             nc.vector.tensor_copy(
                 out=kw[h][:].bitcast(U16).rearrange("p o (a n) -> p a o n", a=2),
                 in_=kw_pairs[h][:].bitcast(U16).rearrange("p (a n o) -> p a o n", a=2, o=PASSES),
             )
-
-        part_words(0)
-        u0_grouped = group_queries("u0", u_raw[0])
-        part_words(1)
-        u_mx = [quantize("u0", u0_grouped[:], NQ), quantize("u1", group_queries("u1", u_raw[1])[:], NQ)]
+        u_grouped = [group_queries(f"u{g}", u_raw[g]) for g in range(PASSES)]
+        u_mx = [quantize(f"u{g}", u_grouped[g][:], NQ) for g in range(PASSES)]
 
         def positions(g, b):
             h, a = divmod(b * BANK_N, HALF)

@@ -11,8 +11,8 @@ BANK_N = 128
 BANKS = SLOTS // BANK_N
 HALF = SLOTS // 2
 RUN = 2
-ROWS_ON_VECTOR = {"v0": 0, "v1": 0, "u0": 0, "u1": 56}
-SLOTS_ON_SCALAR = 192
+ROWS_ON_VECTOR = {"v0": 0, "v1": 0, "u0": 0, "u1": 64}
+SLOTS_ON_SCALAR = 160
 QUARTER = SLOTS // 4
 PLANE_LOADS = ((0, 4), (4, 7), (7, 8))
 ROW_STEP = 8
@@ -107,11 +107,11 @@ def tile_attend_txlseg_kernel(tc, uT, vT, k_words, k_scales, cT, offs, offs2, ou
             nc.vector.tensor_copy(out=ks_both[:, g, :], in_=ks_pool[:, g, :].bitcast(U8).indirect(key_list[:]))
         ks_planes = staged("ks_planes", [P, PASSES, SLOTS // 4], I32)
         nc.vector.tensor_copy(out=ks_planes[:], in_=ks_both[:].bitcast(I32))
-        for r in range(1, 4):
-            nc.sync.dma_start(out=ks_planes[r:P:32], in_=ks_both[r * ROW_STEP : P : 32].bitcast(I32))
         ks = [ks_planes[:, g, :].bitcast(U8) for g in range(PASSES)]
         kw_pool = staged("kw_pool", [P, T], I32)
         nc.sync.dma_start(out=kw_pool[:], in_=k_words[0].rearrange("p t b -> p (t b)").bitcast(I32))
+        for r in range(1, 4):
+            nc.sync.dma_start(out=ks_planes[r:P:32], in_=ks_both[r * ROW_STEP : P : 32].bitcast(I32))
         u_raw = [load_queries("u", uT, g) for g in range(PASSES)]
 
         def position_pass(g, on_scalar, on_vector, shared):

@@ -11,6 +11,7 @@ BANK_N = 128
 BANKS = SLOTS // BANK_N
 HALF = SLOTS // 2
 RUN = 2
+WARM_N = (128, 64)
 ROWS_ON_VECTOR = {"v0": 0, "v1": 0, "u0": 0, "u1": 64}
 SLOTS_ON_SCALAR = 160
 QUARTER = SLOTS // 4
@@ -157,6 +158,19 @@ def tile_attend_txlseg_kernel(tc, uT, vT, k_words, k_scales, cT, offs, offs2, ou
         def keys(g, b):
             h, a = divmod(b * BANK_N, HALF)
             return kw[h][:, g, 2 * a : 2 * (a + BANK_N)].bitcast(FP4X4), ks[g][:, b * BANK_N : (b + 1) * BANK_N]
+
+        warm = psum.tile([P, sum(WARM_N)], F32, name="warm")
+        codes, scales = c_mx[1][0]
+        for a, n in ((0, WARM_N[0]), (WARM_N[0], WARM_N[1])):
+            nc.tensor.matmul_mx(
+                out=warm[:, a : a + n],
+                lhsT=v_mx[1][0][:].bitcast(FP8X4),
+                lhsT_scale=v_mx[1][1][:],
+                rhs=codes[:, a : a + n].bitcast(FP8X4),
+                rhs_scale=scales[:, a : a + n],
+                start=True,
+                stop=True,
+            )
 
         acc = [psum.tile([P, BANK_N], F32, name=f"acc{b}") for b in range(BANKS)]
         passes = [(v_mx[g], positions, g) for g in reversed(range(PASSES))] + [(u_mx[g], keys, g) for g in range(PASSES)]

@@ -10,18 +10,16 @@ PASSES = D // K_PASS
 BANK_N = 128
 BANKS = SLOTS // BANK_N
 HALF = SLOTS // 2
+QUARTER = SLOTS // 4
 RUN = 2
 WARM_N = (128, 64)
-ROWS_ON_VECTOR = {"v0": 0, "v1": 0, "u0": 0, "u1": 64}
+LIST_ROWS = 16
 SLOTS_ON_SCALAR = 160
-QUARTER = SLOTS // 4
 PLANE_LOADS = ((0, 4), (4, 7), (7, 8))
 ROW_STEP = 8
+BURST = 256
 KIB = 1024
-STAGE_AT = {
-    "grouped00": 0, "picked1": 0,
-    "u0_grouped": 3, "u1_grouped": 4, "kw_pairs0": 5, "kw_pairs1": 6,
-}
+STAGE_AT = {"grouped00": 0, "picked1": 0, "u_grouped": 0, "kw_pairs": 4, "v1_codes": 7}
 
 FLOPS = 2 * 2 * D * NQ * SLOTS
 
@@ -42,6 +40,10 @@ def interleave(copy, grouped, planes):
     )
 
 
+def entries(offsets, s0, s1):
+    return offsets[:, s0 // LIST_ROWS : s1 // LIST_ROWS]
+
+
 def tile_attend_txlseg_kernel(tc, uT, vT, k_words, k_scales, cT, offs, offs2, out):
     nc = tc.nc
     with ExitStack() as ctx:
@@ -51,121 +53,103 @@ def tile_attend_txlseg_kernel(tc, uT, vT, k_words, k_scales, cT, offs, offs2, ou
 
         def staged(name, shape, dtype):
             if name not in STAGE_AT:
-                return sb.tile(shape, dtype, name=name, align_bytes=64)
-            return stage.tile(shape, dtype, name=name, offset=int(STAGE_AT[name] * KIB), align_bytes=64)
+                return sb.tile(shape, dtype, name=name, align_bytes=BURST)
+            return stage.tile(shape, dtype, name=name, offset=STAGE_AT[name] * KIB, align_bytes=BURST)
 
+        def quantize(name, grouped, width):
+            codes = staged(f"{name}_codes", [P, width], U32)
+            scales = staged(f"{name}_scales", [P, width], U8)
+            nc.vector.quantize_mx(out=codes[:].bitcast(FP8X4), scales=scales[:], in_=grouped)
+            return codes, scales
+
+        def load_queries(name, queries):
+            raw = staged(f"{name}_raw", [P, PASSES, PACK, NQ], F32)
+            nc.sync.dma_start(out=raw[:], in_=queries[0].rearrange("(g p t) q -> p g t q", p=P, t=PACK))
+            return raw
+
+        def lay_queries(name, raw):
+            grouped = staged(f"{name}_grouped", [P, PASSES, NQ, PACK], BF16)
+            for g in range(PASSES):
+                interleave(nc.scalar.copy, grouped[:, g], raw[:, g])
+            return grouped
+
+        def quantize_queries(name, grouped, g):
+            codes, scales = quantize(f"{name}{g}", grouped[:, g].rearrange("p q t -> p (q t)"), NQ)
+            return codes[:].bitcast(FP8X4), scales[:]
+
+        key_list = sb.tile([P, SLOTS // LIST_ROWS], U16, name="key_list")
+        pos_list = sb.tile([P, SLOTS // LIST_ROWS], U16, name="pos_list")
+        ks_pool = staged("ks_pool", [P, PASSES, T // 4], I32)
+        nc.vector.memset(ks_pool[:], 0)
+        v_raw = load_queries("v", vT)
+        nc.sync.dma_start(key_list[:], offs)
+        nc.sync.dma_start(pos_list[:], offs2)
+        nc.sync.dma_start(out=ks_pool[0:P:ROW_STEP], in_=k_scales.rearrange("o f t -> f o t").bitcast(I32))
         c_rows = cT.rearrange("(g p t) n -> g p t n", p=P, t=PACK)
         windows = {}
-
-        def load_planes(j0, j1):
+        for j0, j1 in PLANE_LOADS:
             planes = staged(f"c{j0}", [P, j1 - j0, C], F32)
             g, t = divmod(j0, PACK)
             nc.sync.dma_start(out=planes[:], in_=c_rows[g, :, t : t + j1 - j0, :])
             for j in range(j0, j1):
                 windows[j] = planes[:, j - j0, :]
+        u_raw = load_queries("u", uT)
+        kw_pool = staged("kw_pool", [P, T], I32)
+        nc.sync.dma_start(out=kw_pool[:], in_=k_words[0].rearrange("p t b -> p (t b)").bitcast(I32))
 
-        def load_queries(name, queries, g):
-            raw = staged(f"{name}{g}_raw", [P, PACK, NQ], F32)
-            nc.sync.dma_start(out=raw[:], in_=queries[0].rearrange("(g p t) q -> g p t q", p=P, t=PACK)[g])
-            return raw
-
-        def quantize(name, grouped, width):
-            codes = staged(f"{name}_codes", [P, width], U32)
-            scales = staged(f"{name}_scales", [P, width], U8)
-            nc.vector.quantize_mx(out=codes[:].bitcast(FP8X4), scales=scales[:], in_=grouped.rearrange("p n t -> p (n t)"))
-            return codes, scales
-
-        def gather_plane(picked, j, s0, s1, on_scalar):
-            dst, src = picked[:, j % PACK, s0:s1], windows[j].indirect(pos_list[:, s0 // 16 : s1 // 16])
-            if on_scalar:
-                nc.scalar.activation(out=dst, in_=src, func=mybir.ActivationFunctionType.Copy)
-            else:
-                nc.vector.tensor_copy(out=dst, in_=src)
-
-        def group_queries(name, raw):
-            cut = ROWS_ON_VECTOR[name]
-            grouped = staged(f"{name}_grouped", [P, NQ, PACK], BF16)
-            interleave(nc.scalar.copy, grouped[:, cut:, :], raw[:, :, cut:])
-            if cut:
-                interleave(nc.vector.tensor_copy, grouped[:, :cut, :], raw[:, :, :cut])
-            return grouped
-
-        key_list = sb.tile([P, SLOTS // 16], U16, name="key_list")
-        pos_list = sb.tile([P, SLOTS // 16], U16, name="pos_list")
-        ks_pool = staged("ks_pool", [P, PASSES, T // 4], I32)
-        nc.vector.memset(ks_pool[:], 0)
-        v_raw = staged("v_raw", [P, PASSES, PACK, NQ], F32)
-        nc.sync.dma_start(out=v_raw[:], in_=vT[0].rearrange("(g p t) q -> p g t q", p=P, t=PACK))
-        nc.sync.dma_start(key_list[:], offs)
-        nc.sync.dma_start(pos_list[:], offs2)
-        nc.sync.dma_start(out=ks_pool[0:P:ROW_STEP], in_=k_scales.rearrange("o f t -> f o t").bitcast(I32))
-        for span in PLANE_LOADS:
-            load_planes(*span)
-
-        v_mx = [quantize(f"v{g}", group_queries(f"v{g}", v_raw[:, g])[:], NQ) for g in range(PASSES)]
+        v_grouped = lay_queries("v", v_raw)
+        v_mx = [quantize_queries("v", v_grouped, 0)]
         ks_both = staged("ks_both", [P, PASSES, SLOTS], U8)
         for g in range(PASSES):
             nc.vector.tensor_copy(out=ks_both[:, g, :], in_=ks_pool[:, g, :].bitcast(U8).indirect(key_list[:]))
         ks_planes = staged("ks_planes", [P, PASSES, SLOTS // 4], I32)
         nc.vector.tensor_copy(out=ks_planes[:], in_=ks_both[:].bitcast(I32))
-        ks = [ks_planes[:, g, :].bitcast(U8) for g in range(PASSES)]
-        kw_pool = staged("kw_pool", [P, T], I32)
-        nc.sync.dma_start(out=kw_pool[:], in_=k_words[0].rearrange("p t b -> p (t b)").bitcast(I32))
         for r in range(1, 4):
             nc.sync.dma_start(out=ks_planes[r:P:32], in_=ks_both[r * ROW_STEP : P : 32].bitcast(I32))
-        u_raw = [load_queries("u", uT, g) for g in range(PASSES)]
 
-        def position_pass(g, on_scalar, on_vector, shared):
+        def gather_plane(picked, j, s0, s1, on_scalar):
+            dst, src = picked[:, j % PACK, s0:s1], windows[j].indirect(entries(pos_list, s0, s1))
+            if on_scalar:
+                nc.scalar.activation(out=dst, in_=src, func=mybir.ActivationFunctionType.Copy)
+            else:
+                nc.vector.tensor_copy(out=dst, in_=src)
+
+        def position_pass(g):
+            first = PACK * g
             picked = staged(f"picked{g}", [P, PACK, SLOTS], F32)
-            gather_plane(picked, on_vector, 0, SLOTS, on_scalar=False)
-            for j in on_scalar:
-                gather_plane(picked, j, 0, SLOTS, on_scalar=True)
-            for j in shared:
-                gather_plane(picked, j, 0, HALF, on_scalar=False)
-                gather_plane(picked, j, HALF, SLOTS, on_scalar=True)
-            last = PACK * g + PACK - 1
-            gather_plane(picked, last, 0, QUARTER, on_scalar=False)
-            gather_plane(picked, last, QUARTER, HALF, on_scalar=True)
-            gather_plane(picked, last, HALF, SLOTS, on_scalar=True)
+            gather_plane(picked, first, 0, SLOTS, on_scalar=False)
+            gather_plane(picked, first + 1, 0, SLOTS, on_scalar=True)
+            gather_plane(picked, first + 2, 0, HALF, on_scalar=False)
+            gather_plane(picked, first + 2, HALF, SLOTS, on_scalar=True)
+            gather_plane(picked, first + 3, 0, QUARTER, on_scalar=False)
+            gather_plane(picked, first + 3, QUARTER, HALF, on_scalar=True)
+            gather_plane(picked, first + 3, HALF, SLOTS, on_scalar=True)
             grouped = [staged(f"grouped{g}{h}", [P, HALF, PACK], BF16) for h in range(2)]
             cut = HALF - SLOTS_ON_SCALAR
             interleave(nc.vector.tensor_copy, grouped[0][:], picked[:, :, :HALF])
             interleave(nc.scalar.copy, grouped[1][:, cut:, :], picked[:, :, HALF + cut :])
             interleave(nc.vector.tensor_copy, grouped[1][:, :cut, :], picked[:, :, HALF : HALF + cut])
-            return [quantize(f"c{g}{h}", grouped[h][:], HALF) for h in range(2)]
+            return grouped
 
-        c_mx = [position_pass(0, (1,), 0, (2,)), position_pass(1, (5,), 4, (6,))]
+        def quantize_positions(g, grouped, h):
+            return quantize(f"c{g}{h}", grouped[h][:].rearrange("p n t -> p (n t)"), HALF)
 
-        kw_pairs = [staged(f"kw_pairs{h}", [P, HALF], U32) for h in range(2)]
-        for h in range(2):
-            nc.vector.tensor_copy(
-                out=kw_pairs[h][:], in_=kw_pool[:].bitcast(U32).indirect(key_list[:, h * HALF // 16 : (h + 1) * HALF // 16])
-            )
-        kw = [staged(f"kw{h}", [P, PASSES, 2 * HALF], U8) for h in range(2)]
-        for h in range(2):
-            nc.vector.tensor_copy(
-                out=kw[h][:].bitcast(U16).rearrange("p o (a n) -> p a o n", a=2),
-                in_=kw_pairs[h][:].bitcast(U16).rearrange("p (a n o) -> p a o n", a=2, o=PASSES),
-            )
-        u_grouped = [group_queries(f"u{g}", u_raw[g]) for g in range(PASSES)]
-        u_mx = [quantize(f"u{g}", u_grouped[g][:], NQ) for g in range(PASSES)]
-
-        def positions(g, b):
-            h, a = divmod(b * BANK_N, HALF)
-            codes, scales = c_mx[g][h]
-            return codes[:, a : a + BANK_N].bitcast(FP8X4), scales[:, a : a + BANK_N]
-
-        def keys(g, b):
-            h, a = divmod(b * BANK_N, HALF)
-            return kw[h][:, g, 2 * a : 2 * (a + BANK_N)].bitcast(FP4X4), ks[g][:, b * BANK_N : (b + 1) * BANK_N]
+        grouped = position_pass(0)
+        c_mx = [[quantize_positions(0, grouped, h) for h in range(2)]]
+        grouped = position_pass(1)
+        first_half = quantize_positions(1, grouped, 0)
+        v_mx.append(quantize_queries("v", v_grouped, 1))
+        c_mx.append([first_half, quantize_positions(1, grouped, 1)])
+        u_grouped = lay_queries("u", u_raw)
+        u_mx = [quantize_queries("u", u_grouped, g) for g in range(PASSES)]
 
         warm = psum.tile([P, sum(WARM_N)], F32, name="warm")
         codes, scales = c_mx[1][0]
         for a, n in ((0, WARM_N[0]), (WARM_N[0], WARM_N[1])):
             nc.tensor.matmul_mx(
                 out=warm[:, a : a + n],
-                lhsT=v_mx[1][0][:].bitcast(FP8X4),
-                lhsT_scale=v_mx[1][1][:],
+                lhsT=v_mx[1][0],
+                lhsT_scale=v_mx[1][1],
                 rhs=codes[:, a : a + n].bitcast(FP8X4),
                 rhs_scale=scales[:, a : a + n],
                 start=True,
@@ -173,19 +157,32 @@ def tile_attend_txlseg_kernel(tc, uT, vT, k_words, k_scales, cT, offs, offs2, ou
             )
 
         acc = [psum.tile([P, BANK_N], F32, name=f"acc{b}") for b in range(BANKS)]
-        passes = [(v_mx[g], positions, g) for g in reversed(range(PASSES))] + [(u_mx[g], keys, g) for g in range(PASSES)]
-        for i, (rows, moving, g) in enumerate(passes):
+
+        def product(b, rows, codes, scales, start, stop):
+            nc.tensor.matmul_mx(
+                out=acc[b][:], lhsT=rows[0], lhsT_scale=rows[1], rhs=codes, rhs_scale=scales, start=start, stop=stop
+            )
+
+        for g in reversed(range(PASSES)):
             for b in range(BANKS):
-                codes, scales = moving(g, b)
-                nc.tensor.matmul_mx(
-                    out=acc[b][:],
-                    lhsT=rows[0][:].bitcast(FP8X4),
-                    lhsT_scale=rows[1][:],
-                    rhs=codes,
-                    rhs_scale=scales,
-                    start=(i == 0),
-                    stop=(i == len(passes) - 1),
-                )
+                h, a = divmod(b * BANK_N, HALF)
+                codes, scales = c_mx[g][h]
+                product(b, v_mx[g], codes[:, a : a + BANK_N].bitcast(FP8X4), scales[:, a : a + BANK_N], g == PASSES - 1, False)
+
+        kw_pairs = staged("kw_pairs", [P, SLOTS], U32)
+        for s0, s1 in ((0, HALF), (HALF, SLOTS)):
+            nc.vector.tensor_copy(out=kw_pairs[:, s0:s1], in_=kw_pool[:].bitcast(U32).indirect(entries(key_list, s0, s1)))
+        kw = [staged(f"kw{b}", [P, PASSES, 2 * BANK_N], U8) for b in range(BANKS)]
+        for b in range(BANKS):
+            nc.vector.tensor_copy(
+                out=kw[b][:].bitcast(U16).rearrange("p o (a n) -> p a o n", a=2),
+                in_=kw_pairs[:, b * BANK_N : (b + 1) * BANK_N].bitcast(U16).rearrange("p (a n o) -> p a o n", a=2, o=PASSES),
+            )
+        for b in range(BANKS):
+            for g in range(PASSES):
+                scales = ks_planes[:, g, :].bitcast(U8)[:, b * BANK_N : (b + 1) * BANK_N]
+                product(b, u_mx[g], kw[b][:, g, :].bitcast(FP4X4), scales, False, g == PASSES - 1)
+
         best = sb.tile([P, SLOTS // SEG], F32, name="best")
         pages = BANK_N // SEG
         for b in range(BANKS):

from contextlib import ExitStack

import concourse.mybir as mybir

P = 128
PACK = 4
K_PASS = P * PACK
D, T, C, NQ, SLOTS, SEG = 1024, 2048, 1024, 128, 512, 32
PASSES = D // K_PASS
BANK_N = 128
BANKS = SLOTS // BANK_N
HALF = SLOTS // 2
QUARTER = SLOTS // 4
RUN = 2
WARM_N = (128, 64)
LIST_ROWS = 16
SLOTS_ON_SCALAR = 160
PLANE_LOADS = ((0, 4), (4, 7), (7, 8))
ROW_STEP = 8
BURST = 256
KIB = 1024
STAGE_AT = {"grouped00": 0, "picked1": 0, "u_grouped": 0, "kw_pairs": 4, "v1_codes": 7}

FLOPS = 2 * 2 * D * NQ * SLOTS

F32 = mybir.dt.float32
BF16 = mybir.dt.bfloat16
I32 = mybir.dt.int32
U32 = mybir.dt.uint32
U16 = mybir.dt.uint16
U8 = mybir.dt.uint8
FP8X4 = mybir.dt.float8_e4m3fn_x4
FP4X4 = mybir.dt.float4_e2m1fn_x4


def interleave(copy, grouped, planes):
    copy(
        out=grouped.rearrange("p (c i) t -> p c t i", i=RUN),
        in_=planes.rearrange("p t (c i) -> p c t i", i=RUN),
    )


def entries(offsets, s0, s1):
    return offsets[:, s0 // LIST_ROWS : s1 // LIST_ROWS]


def tile_attend_txlseg_kernel(tc, uT, vT, k_words, k_scales, cT, offs, offs2, out):
    nc = tc.nc
    with ExitStack() as ctx:
        sb = ctx.enter_context(tc.tile_pool(name="sb", bufs=1))
        stage = ctx.enter_context(tc.tile_pool(name="stage", bufs=1))
        psum = ctx.enter_context(tc.psum_pool(name="psum", bufs=1))

        def staged(name, shape, dtype):
            if name not in STAGE_AT:
                return sb.tile(shape, dtype, name=name, align_bytes=BURST)
            return stage.tile(shape, dtype, name=name, offset=STAGE_AT[name] * KIB, align_bytes=BURST)

        def quantize(name, grouped, width):
            codes = staged(f"{name}_codes", [P, width], U32)
            scales = staged(f"{name}_scales", [P, width], U8)
            nc.vector.quantize_mx(out=codes[:].bitcast(FP8X4), scales=scales[:], in_=grouped)
            return codes, scales

        def load_queries(name, queries):
            raw = staged(f"{name}_raw", [P, PASSES, PACK, NQ], F32)
            nc.sync.dma_start(out=raw[:], in_=queries[0].rearrange("(g p t) q -> p g t q", p=P, t=PACK))
            return raw

        def lay_queries(name, raw):
            grouped = staged(f"{name}_grouped", [P, PASSES, NQ, PACK], BF16)
            for g in range(PASSES):
                interleave(nc.scalar.copy, grouped[:, g], raw[:, g])
            return grouped

        def quantize_queries(name, grouped, g):
            codes, scales = quantize(f"{name}{g}", grouped[:, g].rearrange("p q t -> p (q t)"), NQ)
            return codes[:].bitcast(FP8X4), scales[:]

        key_list = sb.tile([P, SLOTS // LIST_ROWS], U16, name="key_list")
        pos_list = sb.tile([P, SLOTS // LIST_ROWS], U16, name="pos_list")
        ks_pool = staged("ks_pool", [P, PASSES, T // 4], I32)
        nc.vector.memset(ks_pool[:], 0)
        v_raw = load_queries("v", vT)
        nc.sync.dma_start(key_list[:], offs)
        nc.sync.dma_start(pos_list[:], offs2)
        nc.sync.dma_start(out=ks_pool[0:P:ROW_STEP], in_=k_scales.rearrange("o f t -> f o t").bitcast(I32))
        c_rows = cT.rearrange("(g p t) n -> g p t n", p=P, t=PACK)
        windows = {}
        for j0, j1 in PLANE_LOADS:
            planes = staged(f"c{j0}", [P, j1 - j0, C], F32)
            g, t = divmod(j0, PACK)
            nc.sync.dma_start(out=planes[:], in_=c_rows[g, :, t : t + j1 - j0, :])
            for j in range(j0, j1):
                windows[j] = planes[:, j - j0, :]
        u_raw = load_queries("u", uT)
        kw_pool = staged("kw_pool", [P, T], I32)
        nc.sync.dma_start(out=kw_pool[:], in_=k_words[0].rearrange("p t b -> p (t b)").bitcast(I32))

        v_grouped = lay_queries("v", v_raw)
        v_mx = [quantize_queries("v", v_grouped, 0)]
        ks_both = staged("ks_both", [P, PASSES, SLOTS], U8)
        for g in range(PASSES):
            nc.vector.tensor_copy(out=ks_both[:, g, :], in_=ks_pool[:, g, :].bitcast(U8).indirect(key_list[:]))
        ks_planes = staged("ks_planes", [P, PASSES, SLOTS // 4], I32)
        nc.vector.tensor_copy(out=ks_planes[:], in_=ks_both[:].bitcast(I32))
        for r in range(1, 4):
            nc.sync.dma_start(out=ks_planes[r:P:32], in_=ks_both[r * ROW_STEP : P : 32].bitcast(I32))

        def gather_plane(picked, j, s0, s1, on_scalar):
            dst, src = picked[:, j % PACK, s0:s1], windows[j].indirect(entries(pos_list, s0, s1))
            if on_scalar:
                nc.scalar.activation(out=dst, in_=src, func=mybir.ActivationFunctionType.Copy)
            else:
                nc.vector.tensor_copy(out=dst, in_=src)

        def position_pass(g):
            first = PACK * g
            picked = staged(f"picked{g}", [P, PACK, SLOTS], F32)
            gather_plane(picked, first, 0, SLOTS, on_scalar=False)
            gather_plane(picked, first + 1, 0, SLOTS, on_scalar=True)
            gather_plane(picked, first + 2, 0, HALF, on_scalar=False)
            gather_plane(picked, first + 2, HALF, SLOTS, on_scalar=True)
            gather_plane(picked, first + 3, 0, QUARTER, on_scalar=False)
            gather_plane(picked, first + 3, QUARTER, HALF, on_scalar=True)
            gather_plane(picked, first + 3, HALF, SLOTS, on_scalar=True)
            grouped = [staged(f"grouped{g}{h}", [P, HALF, PACK], BF16) for h in range(2)]
            cut = HALF - SLOTS_ON_SCALAR
            interleave(nc.vector.tensor_copy, grouped[0][:], picked[:, :, :HALF])
            interleave(nc.scalar.copy, grouped[1][:, cut:, :], picked[:, :, HALF + cut :])
            interleave(nc.vector.tensor_copy, grouped[1][:, :cut, :], picked[:, :, HALF : HALF + cut])
            return grouped

        def quantize_positions(g, grouped, h):
            return quantize(f"c{g}{h}", grouped[h][:].rearrange("p n t -> p (n t)"), HALF)

        grouped = position_pass(0)
        c_mx = [[quantize_positions(0, grouped, h) for h in range(2)]]
        grouped = position_pass(1)
        first_half = quantize_positions(1, grouped, 0)
        v_mx.append(quantize_queries("v", v_grouped, 1))
        c_mx.append([first_half, quantize_positions(1, grouped, 1)])
        u_grouped = lay_queries("u", u_raw)
        u_mx = [quantize_queries("u", u_grouped, g) for g in range(PASSES)]

        warm = psum.tile([P, sum(WARM_N)], F32, name="warm")
        codes, scales = c_mx[1][0]
        for a, n in ((0, WARM_N[0]), (WARM_N[0], WARM_N[1])):
            nc.tensor.matmul_mx(
                out=warm[:, a : a + n],
                lhsT=v_mx[1][0],
                lhsT_scale=v_mx[1][1],
                rhs=codes[:, a : a + n].bitcast(FP8X4),
                rhs_scale=scales[:, a : a + n],
                start=True,
                stop=True,
            )

        acc = [psum.tile([P, BANK_N], F32, name=f"acc{b}") for b in range(BANKS)]

        def product(b, rows, codes, scales, start, stop):
            nc.tensor.matmul_mx(
                out=acc[b][:], lhsT=rows[0], lhsT_scale=rows[1], rhs=codes, rhs_scale=scales, start=start, stop=stop
            )

        for g in reversed(range(PASSES)):
            for b in range(BANKS):
                h, a = divmod(b * BANK_N, HALF)
                codes, scales = c_mx[g][h]
                product(b, v_mx[g], codes[:, a : a + BANK_N].bitcast(FP8X4), scales[:, a : a + BANK_N], g == PASSES - 1, False)

        kw_pairs = staged("kw_pairs", [P, SLOTS], U32)
        for s0, s1 in ((0, HALF), (HALF, SLOTS)):
            nc.vector.tensor_copy(out=kw_pairs[:, s0:s1], in_=kw_pool[:].bitcast(U32).indirect(entries(key_list, s0, s1)))
        kw = [staged(f"kw{b}", [P, PASSES, 2 * BANK_N], U8) for b in range(BANKS)]
        for b in range(BANKS):
            nc.vector.tensor_copy(
                out=kw[b][:].bitcast(U16).rearrange("p o (a n) -> p a o n", a=2),
                in_=kw_pairs[:, b * BANK_N : (b + 1) * BANK_N].bitcast(U16).rearrange("p (a n o) -> p a o n", a=2, o=PASSES),
            )
        for b in range(BANKS):
            for g in range(PASSES):
                scales = ks_planes[:, g, :].bitcast(U8)[:, b * BANK_N : (b + 1) * BANK_N]
                product(b, u_mx[g], kw[b][:, g, :].bitcast(FP4X4), scales, False, g == PASSES - 1)

        best = sb.tile([P, SLOTS // SEG], F32, name="best")
        pages = BANK_N // SEG
        for b in range(BANKS):
            nc.vector.tensor_reduce(
                out=best[:, b * pages : (b + 1) * pages],
                in_=acc[b][:].rearrange("p (j s) -> p j s", s=SEG),
                axis=mybir.AxisListType.X,
                op=mybir.AluOpType.max,
            )
        nc.sync.dma_start(out=out[0], in_=best[:])
